import numpy as np
import ml_dtypes


def mxq(x, axis, fmt="e4m3"):
    dtype, down = {"e4m3": (ml_dtypes.float8_e4m3fn, 7), "e5m2": (ml_dtypes.float8_e5m2, 14)}[fmt]
    v = np.moveaxis(np.asarray(x, np.float32).astype(ml_dtypes.bfloat16).astype(np.float64), axis, -1)
    blocks = v.reshape(v.shape[:-1] + (-1, 32))
    amax = np.abs(blocks).max(-1, keepdims=True)
    byte = np.maximum(np.where(amax > 0, np.frexp(amax)[1] - 1 + 127, 0) - down, 1)
    scale = np.exp2(byte - 127.0)
    codes = (blocks / scale).astype(np.float32).astype(dtype).astype(np.float64)
    return np.moveaxis((codes * scale).reshape(v.shape), -1, axis)


WIDE = False


def mx_kscale(k):
    if not WIDE:
        return np.ones(k)
    levels = np.array([10, -10, 5, -5, 0])
    if k % 512:
        return np.exp2(np.random.permutation(np.resize(levels, k // 32))).repeat(32)
    a = np.empty((k // 512, 16))
    for p in range(k // 512):
        a[p, :8] = np.random.permutation(np.resize(levels, 8))
        for g in range(8):
            far = levels[np.abs(levels - a[p, g]) >= 10]
            a[p, g + 8] = far[np.random.randint(len(far))]
    return np.exp2(a.ravel()).repeat(32)


def f64(x):
    return np.asarray(x).astype(np.float64)


def striped(idx):
    return np.tile(idx.reshape(-1, 16).T, (8, 1)).astype(np.uint16)


def unstriped(offs):
    return offs[:16].T.reshape(-1).astype(np.int64)


def pack_weight(w):
    k, n = w.shape
    w = f64(np.asarray(w, np.float32).astype(ml_dtypes.bfloat16)).reshape(k // 32, 32, n)
    amax = np.abs(w).max(1)
    byte = np.clip(np.where(amax > 0, np.frexp(amax)[1] - 1 + 127 - 7, 1), 1, 254)
    scaled = (w * np.exp2(127.0 - byte)[:, None, :]).reshape(k, n).astype(np.float32)
    words = np.ascontiguousarray(scaled.reshape(k // 512, 128, 4, n).transpose(0, 1, 3, 2)).astype(ml_dtypes.float8_e4m3fn).view(np.uint8)
    return words, np.ascontiguousarray(byte.astype(np.uint8).reshape(k // 512, 16, n))


def unpack_weight(words, scales):
    g, p, n, _ = words.shape
    vals = np.ascontiguousarray(words).view(ml_dtypes.float8_e4m3fn).astype(np.float64) * np.repeat(np.exp2(scales.astype(np.float64) - 127.0), 8, axis=1)[..., None]
    return vals.transpose(0, 1, 3, 2).reshape(g * 512, n)


def silu(v):
    return v / (1.0 + np.exp(-np.maximum(v, -700.0)))


K, T, S, N, U = 512, 2048, 1024, 128, 1024


def setup_inputs():
    n = np.random.standard_normal
    s = mx_kscale(K)[:, None]
    packed_xT = pack_weight(n((K, T)) * s)
    return {
        "x_words": packed_xT[0],
        "x_scales": packed_xT[1],
        "w1": (n((K, N)) / np.sqrt(K) / s).astype(np.float32),
        "gamma": np.random.uniform(0.5, 1.5, (N, U)).astype(np.float32),
        "beta": (0.5 * n((N, U))).astype(np.float32),
        "offs": striped(np.random.permutation(T)[:S]),
        "cls": striped(np.random.randint(0, U, S)),
    }


def reference(x_words, x_scales, w1, gamma, beta, offs, cls):
    xq = unpack_weight(x_words, x_scales)[:, unstriped(offs)]
    y = mxq(f64(w1), 0, "e4m3").T @ xq
    g = f64(gamma)[:, unstriped(cls)]
    s = f64(beta)[:, unstriped(cls)]
    return silu(y * g + s)

@@ -1,0 +1,100 @@
+from contextlib import ExitStack
+
+import concourse.mybir as mybir
+
+F32 = mybir.dt.float32
+BF16 = mybir.dt.bfloat16
+I32 = mybir.dt.int32
+U32 = mybir.dt.uint32
+U16 = mybir.dt.uint16
+U8 = mybir.dt.uint8
+FP8X4 = mybir.dt.float8_e4m3fn_x4
+MULT = mybir.AluOpType.mult
+ADD = mybir.AluOpType.add
+SILU = mybir.ActivationFunctionType.Silu
+
+P = 128
+PACK = 4
+K, T, S, N, U = 512, 2048, 1024, 128, 1024
+HALF = 512
+QUARTER = 256
+STRIPE = 16
+FLOPS = 2 * K * N * S
+PIECES = ((0, 512), (512, 768), (768, 1024))
+SCALE_PIECES = ((0, 256), (256, 512), (512, 1024))
+
+
+def entries(offsets, lo, hi):
+    return offsets[:, lo // STRIPE : hi // STRIPE]
+
+
+def tile_picked_cbn_silu_p_kernel(tc, x_words, x_scales, w1, gamma, beta, offs, cls, out):
+    nc = tc.nc
+    with ExitStack() as ctx:
+        sb = ctx.enter_context(tc.tile_pool(name="sb", bufs=1))
+        psum = ctx.enter_context(tc.psum_pool(name="psum", bufs=1))
+
+        offs_sb = sb.tile([P, S // STRIPE], U16)
+        cls_sb = sb.tile([P, S // STRIPE], U16)
+        scale_table = sb.tile([P, T], U8, align_bytes=64)
+        word_table = sb.tile([P, T], I32, align_bytes=64)
+        w_raw = sb.tile([P, PACK, N], F32, align_bytes=64)
+        gamma_sb = sb.tile([P, U], F32, align_bytes=64)
+        beta_sb = sb.tile([P, U], F32, align_bytes=64)
+
+        nc.sync.dma_start(offs_sb[:], offs)
+        for q in range(4):
+            rows = x_scales[0][4 * q : 4 * q + 4, :].bitcast(I32)
+            nc.sync.dma_start(
+                scale_table[32 * q : 32 * q + 32, :].bitcast(I32), rows.unsqueeze(0).to_broadcast([8, 4, T // 4])
+            )
+        nc.sync.dma_start(w_raw[:], w1.rearrange("(p j) m -> p j m", j=PACK))
+        nc.sync.dma_start(word_table[:], x_words[0].rearrange("p c t -> p (c t)").bitcast(I32))
+        nc.sync.dma_start(cls_sb[:], cls)
+        nc.sync.dma_start(gamma_sb[:], gamma)
+        nc.sync.dma_start(beta_sb[:], beta)
+
+        warm = sb.tile([P, 1], F32)
+        warm_out = sb.tile([P, 1], F32)
+        nc.gpsimd.memset(warm[:], 0.0)
+        nc.scalar.activation(warm_out[:], warm[:], SILU)
+
+        w_grouped = sb.tile([P, N, PACK], BF16, align_bytes=64)
+        w_codes = sb.tile([P, N], U32, align_bytes=64)
+        w_scales = sb.tile([P, N], U8, align_bytes=64)
+        nc.scalar.copy(w_grouped[:], w_raw[:].rearrange("p j m -> p m j"))
+
+        picked_scales = sb.tile([P, S], U8, align_bytes=64)
+        nc.vector.tensor_copy(picked_scales[:], scale_table[:].indirect(offs_sb[:]))
+        nc.vector.quantize_mx(
+            out=w_codes[:].bitcast(FP8X4), scales=w_scales[:], in_=w_grouped[:].rearrange("p m j -> p (m j)")
+        )
+
+        y = sb.tile([P, S], F32, align_bytes=64)
+        for h in range(S // HALF):
+            lo, hi = h * HALF, (h + 1) * HALF
+            picked_words = sb.tile([P, HALF], U32, align_bytes=64, name="picked_words%d" % h)
+            nc.vector.tensor_copy(picked_words[:], word_table[:].bitcast(U32).indirect(entries(offs_sb, lo, hi)))
+            for a in range(lo, hi, QUARTER):
+                acc = psum.tile([P, QUARTER], F32, name="acc%d" % a)
+                nc.tensor.matmul_mx(
+                    out=acc[:],
+                    lhsT=w_codes[:].bitcast(FP8X4),
+                    lhsT_scale=w_scales[:],
+                    rhs=picked_words[:, a - lo : a - lo + QUARTER].bitcast(FP8X4),
+                    rhs_scale=picked_scales[:, a : a + QUARTER],
+                    start=True,
+                    stop=True,
+                )
+                nc.scalar.copy(y[:, a : a + QUARTER], acc[:])
+
+        scaled = sb.tile([P, S], F32, align_bytes=64)
+        for lo, hi in SCALE_PIECES:
+            nc.vector.tensor_tensor(scaled[:, lo:hi], gamma_sb[:].indirect(entries(cls_sb, lo, hi)), y[:, lo:hi], MULT)
+
+        shifted = sb.tile([P, S], F32, align_bytes=64)
+        result = sb.tile([P, S], F32, align_bytes=64)
+        for lo, hi in PIECES:
+            nc.vector.tensor_tensor(shifted[:, lo:hi], beta_sb[:].indirect(entries(cls_sb, lo, hi)), scaled[:, lo:hi], ADD)
+            nc.scalar.activation(result[:, lo:hi], shifted[:, lo:hi], SILU)
+            nc.sync.dma_start(out[:, lo:hi], result[:, lo:hi])

@@ -20,8 +20,8 @@ HALF = 512
 QUARTER = 256
 STRIPE = 16
 FLOPS = 2 * K * N * S
-PIECES = ((0, 512), (512, 768), (768, 1024))
-SCALE_PIECES = ((0, 256), (256, 512), (512, 1024))
+PIECES = ((0, 512), (512, 832), (832, 1024))
+SCALE_PIECES = ((0, 512), (512, 1024))
 
 
 def entries(offsets, lo, hi):
@@ -42,13 +42,11 @@ def tile_picked_cbn_silu_p_kernel(tc, x_words, x_scales, w1, gamma, beta, offs, 
         gamma_sb = sb.tile([P, U], F32, align_bytes=64)
         beta_sb = sb.tile([P, U], F32, align_bytes=64)
 
+        nc.vector.memset(scale_table[:].bitcast(I32), 0)
         nc.sync.dma_start(offs_sb[:], offs)
-        for q in range(4):
-            rows = x_scales[0][4 * q : 4 * q + 4, :].bitcast(I32)
-            nc.sync.dma_start(
-                scale_table[32 * q : 32 * q + 32, :].bitcast(I32), rows.unsqueeze(0).to_broadcast([8, 4, T // 4])
-            )
         nc.sync.dma_start(w_raw[:], w1.rearrange("(p j) m -> p j m", j=PACK))
+        for r in range(4):
+            nc.sync.dma_start(scale_table[r:P:32, :].bitcast(I32), x_scales[0][r:16:4, :].bitcast(I32))
         nc.sync.dma_start(word_table[:], x_words[0].rearrange("p c t -> p (c t)").bitcast(I32))
         nc.sync.dma_start(cls_sb[:], cls)
         nc.sync.dma_start(gamma_sb[:], gamma)
@@ -62,13 +60,15 @@ def tile_picked_cbn_silu_p_kernel(tc, x_words, x_scales, w1, gamma, beta, offs, 
         w_grouped = sb.tile([P, N, PACK], BF16, align_bytes=64)
         w_codes = sb.tile([P, N], U32, align_bytes=64)
         w_scales = sb.tile([P, N], U8, align_bytes=64)
-        nc.scalar.copy(w_grouped[:], w_raw[:].rearrange("p j m -> p m j"))
-
-        picked_scales = sb.tile([P, S], U8, align_bytes=64)
-        nc.vector.tensor_copy(picked_scales[:], scale_table[:].indirect(offs_sb[:]))
+        nc.vector.tensor_copy(
+            w_grouped[:].rearrange("p (c i) j -> p c j i", i=4), w_raw[:].rearrange("p j (c i) -> p c j i", i=4)
+        )
         nc.vector.quantize_mx(
             out=w_codes[:].bitcast(FP8X4), scales=w_scales[:], in_=w_grouped[:].rearrange("p m j -> p (m j)")
         )
+
+        picked_scales = sb.tile([P, S], U8, align_bytes=64)
+        nc.vector.tensor_copy(picked_scales[:], scale_table[:].indirect(offs_sb[:]))
 
         y = sb.tile([P, S], F32, align_bytes=64)
         for h in range(S // HALF):

@@ -16,7 +16,7 @@ SILU = mybir.ActivationFunctionType.Silu
 P = 128
 PACK = 4
 K, T, S, N, U = 512, 2048, 1024, 128, 1024
-HALF = 512
+HALF = 256
 QUARTER = 256
 STRIPE = 16
 FLOPS = 2 * K * N * S
@@ -43,19 +43,14 @@ def tile_picked_cbn_silu_p_kernel(tc, x_words, x_scales, w1, gamma, beta, offs, 
         beta_sb = sb.tile([P, U], F32, align_bytes=64)
 
         nc.vector.memset(scale_table[:].bitcast(I32), 0)
-        nc.sync.dma_start(offs_sb[:], offs)
         nc.sync.dma_start(w_raw[:], w1.rearrange("(p j) m -> p j m", j=PACK))
+        nc.sync.dma_start(offs_sb[:], offs)
         for r in range(4):
             nc.sync.dma_start(scale_table[r:P:32, :].bitcast(I32), x_scales[0][r:16:4, :].bitcast(I32))
         nc.sync.dma_start(word_table[:], x_words[0].rearrange("p c t -> p (c t)").bitcast(I32))
         nc.sync.dma_start(cls_sb[:], cls)
         nc.sync.dma_start(gamma_sb[:], gamma)
         nc.sync.dma_start(beta_sb[:], beta)
-
-        warm = sb.tile([P, 1], F32)
-        warm_out = sb.tile([P, 1], F32)
-        nc.gpsimd.memset(warm[:], 0.0)
-        nc.scalar.activation(warm_out[:], warm[:], SILU)
 
         w_grouped = sb.tile([P, N, PACK], BF16, align_bytes=64)
         w_codes = sb.tile([P, N], U32, align_bytes=64)

@@ -84,12 +84,21 @@ def tile_picked_cbn_silu_p_kernel(tc, x_words, x_scales, w1, gamma, beta, offs, 
                 nc.scalar.copy(y[:, a : a + QUARTER], acc[:])
 
         scaled = sb.tile([P, S], F32, align_bytes=64)
-        for lo, hi in SCALE_PIECES:
-            nc.vector.tensor_tensor(scaled[:, lo:hi], gamma_sb[:].indirect(entries(cls_sb, lo, hi)), y[:, lo:hi], MULT)
-
         shifted = sb.tile([P, S], F32, align_bytes=64)
         result = sb.tile([P, S], F32, align_bytes=64)
-        for lo, hi in PIECES:
+
+        def scale(lo, hi):
+            nc.vector.tensor_tensor(scaled[:, lo:hi], gamma_sb[:].indirect(entries(cls_sb, lo, hi)), y[:, lo:hi], MULT)
+
+        def shift(lo, hi):
             nc.vector.tensor_tensor(shifted[:, lo:hi], beta_sb[:].indirect(entries(cls_sb, lo, hi)), scaled[:, lo:hi], ADD)
             nc.scalar.activation(result[:, lo:hi], shifted[:, lo:hi], SILU)
             nc.sync.dma_start(out[:, lo:hi], result[:, lo:hi])
+
+        scale(0, 512)
+        scale(512, 768)
+        shift(0, 512)
+        scale(768, 1024)
+        shift(512, 768)
+        shift(768, 928)
+        shift(928, 1024)

@@ -16,12 +16,8 @@ SILU = mybir.ActivationFunctionType.Silu
 P = 128
 PACK = 4
 K, T, S, N, U = 512, 2048, 1024, 128, 1024
-HALF = 256
-QUARTER = 256
 STRIPE = 16
 FLOPS = 2 * K * N * S
-PIECES = ((0, 512), (512, 832), (832, 1024))
-SCALE_PIECES = ((0, 512), (512, 1024))
 
 
 def entries(offsets, lo, hi):
@@ -36,69 +32,101 @@ def tile_picked_cbn_silu_p_kernel(tc, x_words, x_scales, w1, gamma, beta, offs, 
 
         offs_sb = sb.tile([P, S // STRIPE], U16)
         cls_sb = sb.tile([P, S // STRIPE], U16)
-        scale_table = sb.tile([P, T], U8, align_bytes=64)
+        scale_table = sb.tile([P, T], U8, align_bytes=64, tag="scale_then_beta")
         word_table = sb.tile([P, T], I32, align_bytes=64)
         w_raw = sb.tile([P, PACK, N], F32, align_bytes=64)
         gamma_sb = sb.tile([P, U], F32, align_bytes=64)
-        beta_sb = sb.tile([P, U], F32, align_bytes=64)
-
-        nc.vector.memset(scale_table[:].bitcast(I32), 0)
-        nc.sync.dma_start(w_raw[:], w1.rearrange("(p j) m -> p j m", j=PACK))
-        nc.sync.dma_start(offs_sb[:], offs)
-        for r in range(4):
-            nc.sync.dma_start(scale_table[r:P:32, :].bitcast(I32), x_scales[0][r:16:4, :].bitcast(I32))
-        nc.sync.dma_start(word_table[:], x_words[0].rearrange("p c t -> p (c t)").bitcast(I32))
-        nc.sync.dma_start(cls_sb[:], cls)
-        nc.sync.dma_start(gamma_sb[:], gamma)
-        nc.sync.dma_start(beta_sb[:], beta)
-
         w_grouped = sb.tile([P, N, PACK], BF16, align_bytes=64)
         w_codes = sb.tile([P, N], U32, align_bytes=64)
         w_scales = sb.tile([P, N], U8, align_bytes=64)
-        nc.vector.tensor_copy(
-            w_grouped[:].rearrange("p (c i) j -> p c j i", i=4), w_raw[:].rearrange("p j (c i) -> p c j i", i=4)
-        )
-        nc.vector.quantize_mx(
-            out=w_codes[:].bitcast(FP8X4), scales=w_scales[:], in_=w_grouped[:].rearrange("p m j -> p (m j)")
-        )
-
-        picked_scales = sb.tile([P, S], U8, align_bytes=64)
-        nc.vector.tensor_copy(picked_scales[:], scale_table[:].indirect(offs_sb[:]))
-
+        plane = sb.tile([P, S], U8, align_bytes=64)
+        picked_scales = {}
         y = sb.tile([P, S], F32, align_bytes=64)
-        for h in range(S // HALF):
-            lo, hi = h * HALF, (h + 1) * HALF
-            picked_words = sb.tile([P, HALF], U32, align_bytes=64, name="picked_words%d" % h)
-            nc.vector.tensor_copy(picked_words[:], word_table[:].bitcast(U32).indirect(entries(offs_sb, lo, hi)))
-            for a in range(lo, hi, QUARTER):
-                acc = psum.tile([P, QUARTER], F32, name="acc%d" % a)
-                nc.tensor.matmul_mx(
-                    out=acc[:],
-                    lhsT=w_codes[:].bitcast(FP8X4),
-                    lhsT_scale=w_scales[:],
-                    rhs=picked_words[:, a - lo : a - lo + QUARTER].bitcast(FP8X4),
-                    rhs_scale=picked_scales[:, a : a + QUARTER],
-                    start=True,
-                    stop=True,
-                )
-                nc.scalar.copy(y[:, a : a + QUARTER], acc[:])
-
         scaled = sb.tile([P, S], F32, align_bytes=64)
         shifted = sb.tile([P, S], F32, align_bytes=64)
         result = sb.tile([P, S], F32, align_bytes=64)
+        words_in = x_words[0].rearrange("p c t -> p (c t)").bitcast(I32)
+        picked_words = {}
+
+        def load_scale_rows(r, queue):
+            queue.dma_start(scale_table[r:P:32, :].bitcast(I32), x_scales[0][r:16:4, :].bitcast(I32))
+
+        def cast_w(copy):
+            copy(
+                w_grouped[:].rearrange("p (c i) j -> p c j i", i=4), w_raw[:].rearrange("p j (c i) -> p c j i", i=4)
+            )
+
+        def quantise_w():
+            nc.vector.quantize_mx(
+                out=w_codes[:].bitcast(FP8X4), scales=w_scales[:], in_=w_grouped[:].rearrange("p m j -> p (m j)")
+            )
+
+        def pick_scales(lo, hi):
+            picked_scales[lo] = sb.tile([P, hi - lo], U8, align_bytes=64, name="picked_scales%d" % lo)
+            nc.vector.tensor_copy(picked_scales[lo][:], scale_table[:].indirect(entries(offs_sb, lo, hi)))
+
+        def place_scales(lo, hi, queue):
+            for r in range(4):
+                queue.dma_start(plane[r:P:32, lo:hi].bitcast(I32), picked_scales[lo][8 * r : P : 32, :].bitcast(I32))
+
+        def words_tile(base, end, tag):
+            picked_words[base] = sb.tile([P, end - base], U32, align_bytes=64, name="picked_words%d" % base, tag=tag)
+
+        def pick_words(base, lo, hi):
+            nc.vector.tensor_copy(
+                picked_words[base][:, lo - base : hi - base], word_table[:].bitcast(U32).indirect(entries(offs_sb, lo, hi))
+            )
+
+        def product(base, lo, hi):
+            acc = psum.tile([P, hi - lo], F32, name="acc%d" % lo)
+            nc.tensor.matmul_mx(
+                out=acc[:],
+                lhsT=w_codes[:].bitcast(FP8X4),
+                lhsT_scale=w_scales[:],
+                rhs=picked_words[base][:, lo - base : hi - base].bitcast(FP8X4),
+                rhs_scale=plane[:, lo:hi],
+                start=True,
+                stop=True,
+            )
+            nc.scalar.copy(y[:, lo:hi], acc[:])
 
         def scale(lo, hi):
             nc.vector.tensor_tensor(scaled[:, lo:hi], gamma_sb[:].indirect(entries(cls_sb, lo, hi)), y[:, lo:hi], MULT)
 
-        def shift(lo, hi):
+        def shift(lo, hi, queue):
             nc.vector.tensor_tensor(shifted[:, lo:hi], beta_sb[:].indirect(entries(cls_sb, lo, hi)), scaled[:, lo:hi], ADD)
             nc.scalar.activation(result[:, lo:hi], shifted[:, lo:hi], SILU)
-            nc.sync.dma_start(out[:, lo:hi], result[:, lo:hi])
+            queue.dma_start(out[:, lo:hi], result[:, lo:hi])
 
+        nc.vector.memset(scale_table[:].bitcast(I32), 0)
+        nc.sync.dma_start(w_raw[:], w1.rearrange("(p j) m -> p j m", j=PACK))
+        nc.sync.dma_start(offs_sb[:], offs)
+        nc.sync.dma_start(scale_table[0:P:8, :].bitcast(I32), x_scales[0].bitcast(I32))
+        nc.sync.dma_start(word_table[:], words_in)
+        nc.sync.dma_start(cls_sb[:], cls)
+        nc.sync.dma_start(gamma_sb[:], gamma)
+        cast_w(nc.scalar.copy)
+        pick_scales(0, 512)
+        place_scales(0, 512, nc.sync)
+        pick_scales(512, S)
+        place_scales(512, S, nc.sync)
+        quantise_w()
+        beta_sb = sb.tile([P, U], F32, align_bytes=64, tag="scale_then_beta")
+        nc.sync.dma_start(beta_sb[:], beta)
+        words_tile(0, 512, "early")
+        pick_words(0, 0, 256)
+        product(0, 0, 256)
+        pick_words(0, 256, 512)
+        product(0, 256, 512)
+        words_tile(512, 1024, "late")
+        pick_words(512, 512, 768)
+        product(512, 512, 768)
+        pick_words(512, 768, 1024)
+        product(512, 768, 1024)
         scale(0, 512)
         scale(512, 768)
-        shift(0, 512)
+        shift(0, 512, nc.sync)
         scale(768, 1024)
-        shift(512, 768)
-        shift(768, 928)
-        shift(928, 1024)
+        shift(512, 768, nc.sync)
+        shift(768, 928, nc.sync)
+        shift(928, 1024, nc.sync)

@@ -48,8 +48,9 @@ def tile_picked_cbn_silu_p_kernel(tc, x_words, x_scales, w1, gamma, beta, offs, 
         words_in = x_words[0].rearrange("p c t -> p (c t)").bitcast(I32)
         picked_words = {}
 
-        def load_scale_rows(r, queue):
-            queue.dma_start(scale_table[r:P:32, :].bitcast(I32), x_scales[0][r:16:4, :].bitcast(I32))
+        def load_scale_rows(u, queue):
+            rows = x_scales[0].bitcast(I32).rearrange("(h u r) c -> u r h c", h=2, u=2)
+            queue.dma_start(scale_table[64 * u : 64 * u + 8, :].bitcast(I32), rows[u])
 
         def cast_w(copy):
             copy(
@@ -66,8 +67,10 @@ def tile_picked_cbn_silu_p_kernel(tc, x_words, x_scales, w1, gamma, beta, offs, 
             nc.vector.tensor_copy(picked_scales[lo][:], scale_table[:].indirect(entries(offs_sb, lo, hi)))
 
         def place_scales(lo, hi, queue):
-            for r in range(4):
-                queue.dma_start(plane[r:P:32, lo:hi].bitcast(I32), picked_scales[lo][8 * r : P : 32, :].bitcast(I32))
+            for h in range(2):
+                queue.dma_start(
+                    plane[64 * h : 64 * h + 64, lo:hi].bitcast(I32), picked_scales[lo][h:P:2, :].bitcast(I32)
+                )
 
         def words_tile(base, end, tag):
             picked_words[base] = sb.tile([P, end - base], U32, align_bytes=64, name="picked_words%d" % base, tag=tag)
@@ -101,32 +104,34 @@ def tile_picked_cbn_silu_p_kernel(tc, x_words, x_scales, w1, gamma, beta, offs, 
         nc.vector.memset(scale_table[:].bitcast(I32), 0)
         nc.sync.dma_start(w_raw[:], w1.rearrange("(p j) m -> p j m", j=PACK))
         nc.sync.dma_start(offs_sb[:], offs)
-        nc.sync.dma_start(scale_table[0:P:8, :].bitcast(I32), x_scales[0].bitcast(I32))
+        load_scale_rows(0, nc.sync)
+        load_scale_rows(1, nc.sync)
         nc.sync.dma_start(word_table[:], words_in)
         nc.sync.dma_start(cls_sb[:], cls)
         nc.sync.dma_start(gamma_sb[:], gamma)
         cast_w(nc.scalar.copy)
-        pick_scales(0, 512)
-        place_scales(0, 512, nc.sync)
-        pick_scales(512, S)
-        place_scales(512, S, nc.sync)
+        pick_scales(0, 640)
+        place_scales(0, 640, nc.sync)
+        pick_scales(640, S)
+        place_scales(640, S, nc.sync)
         quantise_w()
         beta_sb = sb.tile([P, U], F32, align_bytes=64, tag="scale_then_beta")
         nc.sync.dma_start(beta_sb[:], beta)
-        words_tile(0, 512, "early")
+        words_tile(0, 256, "a")
         pick_words(0, 0, 256)
         product(0, 0, 256)
-        pick_words(0, 256, 512)
-        product(0, 256, 512)
-        words_tile(512, 1024, "late")
-        pick_words(512, 512, 768)
-        product(512, 512, 768)
-        pick_words(512, 768, 1024)
-        product(512, 768, 1024)
-        scale(0, 512)
-        scale(512, 768)
-        shift(0, 512, nc.sync)
-        scale(768, 1024)
-        shift(512, 768, nc.sync)
-        shift(768, 928, nc.sync)
+        words_tile(256, 640, "b")
+        pick_words(256, 256, 640)
+        product(256, 256, 512)
+        product(256, 512, 640)
+        words_tile(640, 1024, "c")
+        pick_words(640, 640, 1024)
+        product(640, 640, 896)
+        product(640, 896, 1024)
+        scale(0, 256)
+        scale(256, 640)
+        scale(640, 1024)
+        shift(0, 384, nc.sync)
+        shift(384, 736, nc.sync)
+        shift(736, 928, nc.sync)
         shift(928, 1024, nc.sync)

@@ -34,8 +34,7 @@ def tile_picked_cbn_silu_p_kernel(tc, x_words, x_scales, w1, gamma, beta, offs, 
         cls_sb = sb.tile([P, S // STRIPE], U16)
         scale_table = sb.tile([P, T], U8, align_bytes=64, tag="scale_then_beta")
         word_table = sb.tile([P, T], I32, align_bytes=64)
-        w_raw = sb.tile([P, PACK, N], F32, align_bytes=64)
-        gamma_sb = sb.tile([P, U], F32, align_bytes=64)
+        w_raw = sb.tile([P, PACK, N], F32, align_bytes=64, tag="w_then_gamma")
         w_grouped = sb.tile([P, N, PACK], BF16, align_bytes=64)
         w_codes = sb.tile([P, N], U32, align_bytes=64)
         w_scales = sb.tile([P, N], U8, align_bytes=64)
@@ -50,7 +49,7 @@ def tile_picked_cbn_silu_p_kernel(tc, x_words, x_scales, w1, gamma, beta, offs, 
 
         def load_scale_rows(u, queue):
             rows = x_scales[0].bitcast(I32).rearrange("(h u r) c -> u r h c", h=2, u=2)
-            queue.dma_start(scale_table[64 * u : 64 * u + 8, :].bitcast(I32), rows[u])
+            queue.dma_start(scale_table[64 * u + 24 : 64 * u + 32, :].bitcast(I32), rows[u])
 
         def cast_w(copy):
             copy(
@@ -87,7 +86,7 @@ def tile_picked_cbn_silu_p_kernel(tc, x_words, x_scales, w1, gamma, beta, offs, 
                 lhsT=w_codes[:].bitcast(FP8X4),
                 lhsT_scale=w_scales[:],
                 rhs=picked_words[base][:, lo - base : hi - base].bitcast(FP8X4),
-                rhs_scale=plane[:, lo:hi],
+                rhs_scale=plane[12:P, lo:hi],
                 start=True,
                 stop=True,
             )
@@ -101,36 +100,40 @@ def tile_picked_cbn_silu_p_kernel(tc, x_words, x_scales, w1, gamma, beta, offs, 
             nc.scalar.activation(result[:, lo:hi], shifted[:, lo:hi], SILU)
             queue.dma_start(out[:, lo:hi], result[:, lo:hi])
 
-        nc.vector.memset(scale_table[:].bitcast(I32), 0)
-        nc.sync.dma_start(w_raw[:], w1.rearrange("(p j) m -> p j m", j=PACK))
         nc.sync.dma_start(offs_sb[:], offs)
         load_scale_rows(0, nc.sync)
         load_scale_rows(1, nc.sync)
+        nc.vector.memset(scale_table[0:24, :].bitcast(I32), 0)
+        nc.gpsimd.memset(scale_table[32:64, :].bitcast(I32), 0)
+        nc.vector.memset(scale_table[64:88, :].bitcast(I32), 0)
+        nc.gpsimd.memset(scale_table[96:P, :].bitcast(I32), 0)
+        nc.sync.dma_start(w_raw[:], w1.rearrange("(p j) m -> p j m", j=PACK))
         nc.sync.dma_start(word_table[:], words_in)
         nc.sync.dma_start(cls_sb[:], cls)
-        nc.sync.dma_start(gamma_sb[:], gamma)
         cast_w(nc.scalar.copy)
-        pick_scales(0, 640)
-        place_scales(0, 640, nc.sync)
-        pick_scales(640, S)
-        place_scales(640, S, nc.sync)
+        gamma_sb = sb.tile([P, U], F32, align_bytes=64, tag="w_then_gamma")
+        nc.scalar.dma_start(gamma_sb[:], gamma)
+        pick_scales(0, 384)
+        place_scales(0, 384, nc.sync)
+        pick_scales(384, S)
+        place_scales(384, S, nc.sync)
         quantise_w()
         beta_sb = sb.tile([P, U], F32, align_bytes=64, tag="scale_then_beta")
         nc.sync.dma_start(beta_sb[:], beta)
-        words_tile(0, 256, "a")
-        pick_words(0, 0, 256)
+        words_tile(0, 384, "a")
+        pick_words(0, 0, 384)
         product(0, 0, 256)
-        words_tile(256, 640, "b")
-        pick_words(256, 256, 640)
-        product(256, 256, 512)
-        product(256, 512, 640)
-        words_tile(640, 1024, "c")
-        pick_words(640, 640, 1024)
-        product(640, 640, 896)
-        product(640, 896, 1024)
-        scale(0, 256)
-        scale(256, 640)
-        scale(640, 1024)
+        product(0, 256, 384)
+        words_tile(384, 768, "b")
+        pick_words(384, 384, 768)
+        product(384, 384, 640)
+        product(384, 640, 768)
+        words_tile(768, 1024, "c")
+        pick_words(768, 768, 1024)
+        product(768, 768, 1024)
+        scale(0, 384)
+        scale(384, 768)
+        scale(768, 1024)
         shift(0, 384, nc.sync)
         shift(384, 736, nc.sync)
         shift(736, 928, nc.sync)

@@ -28,13 +28,14 @@ def tile_picked_cbn_silu_p_kernel(tc, x_words, x_scales, w1, gamma, beta, offs, 
     nc = tc.nc
     with ExitStack() as ctx:
         sb = ctx.enter_context(tc.tile_pool(name="sb", bufs=1))
+        reuse = ctx.enter_context(tc.tile_pool(name="reuse", bufs=1))
         psum = ctx.enter_context(tc.psum_pool(name="psum", bufs=1))
 
         offs_sb = sb.tile([P, S // STRIPE], U16)
         cls_sb = sb.tile([P, S // STRIPE], U16)
         scale_table = sb.tile([P, T], U8, align_bytes=64, tag="scale_then_beta")
         word_table = sb.tile([P, T], I32, align_bytes=64)
-        w_raw = sb.tile([P, PACK, N], F32, align_bytes=64, tag="w_then_gamma")
+        w_raw = reuse.tile([P, PACK, N], F32, align_bytes=64, offset=0)
         w_grouped = sb.tile([P, N, PACK], BF16, align_bytes=64)
         w_codes = sb.tile([P, N], U32, align_bytes=64)
         w_scales = sb.tile([P, N], U8, align_bytes=64)
@@ -61,8 +62,8 @@ def tile_picked_cbn_silu_p_kernel(tc, x_words, x_scales, w1, gamma, beta, offs, 
                 out=w_codes[:].bitcast(FP8X4), scales=w_scales[:], in_=w_grouped[:].rearrange("p m j -> p (m j)")
             )
 
-        def pick_scales(lo, hi):
-            picked_scales[lo] = sb.tile([P, hi - lo], U8, align_bytes=64, name="picked_scales%d" % lo)
+        def pick_scales(lo, hi, picked):
+            picked_scales[lo] = picked
             nc.vector.tensor_copy(picked_scales[lo][:], scale_table[:].indirect(entries(offs_sb, lo, hi)))
 
         def place_scales(lo, hi, queue):
@@ -111,30 +112,32 @@ def tile_picked_cbn_silu_p_kernel(tc, x_words, x_scales, w1, gamma, beta, offs, 
         nc.sync.dma_start(word_table[:], words_in)
         nc.sync.dma_start(cls_sb[:], cls)
         cast_w(nc.scalar.copy)
-        gamma_sb = sb.tile([P, U], F32, align_bytes=64, tag="w_then_gamma")
-        nc.scalar.dma_start(gamma_sb[:], gamma)
-        pick_scales(0, 384)
-        place_scales(0, 384, nc.sync)
-        pick_scales(384, S)
-        place_scales(384, S, nc.sync)
+        gamma_sb = reuse.tile([P, U], F32, align_bytes=64, offset=1024)
+        nc.sync.dma_start(gamma_sb[:], gamma)
+        first_scales = sb.tile([P, 640], U8, align_bytes=64)
+        pick_scales(0, 640, first_scales)
+        place_scales(0, 640, nc.sync)
+        second_scales = reuse.tile([P, S - 640], U8, align_bytes=64, offset=0)
+        pick_scales(640, S, second_scales)
+        place_scales(640, S, nc.sync)
         quantise_w()
         beta_sb = sb.tile([P, U], F32, align_bytes=64, tag="scale_then_beta")
         nc.sync.dma_start(beta_sb[:], beta)
-        words_tile(0, 384, "a")
-        pick_words(0, 0, 384)
+        words_tile(0, 256, "a")
+        pick_words(0, 0, 256)
         product(0, 0, 256)
-        product(0, 256, 384)
-        words_tile(384, 768, "b")
-        pick_words(384, 384, 768)
-        product(384, 384, 640)
-        product(384, 640, 768)
-        words_tile(768, 1024, "c")
-        pick_words(768, 768, 1024)
-        product(768, 768, 1024)
-        scale(0, 384)
-        scale(384, 768)
-        scale(768, 1024)
-        shift(0, 384, nc.sync)
-        shift(384, 736, nc.sync)
-        shift(736, 928, nc.sync)
-        shift(928, 1024, nc.sync)
+        words_tile(256, 640, "b")
+        pick_words(256, 256, 640)
+        product(256, 256, 512)
+        product(256, 512, 640)
+        words_tile(640, 1024, "c")
+        pick_words(640, 640, 1024)
+        product(640, 640, 896)
+        product(640, 896, 1024)
+        scale(0, 256)
+        scale(256, 640)
+        shift(0, 256, nc.sync)
+        scale(640, 1024)
+        shift(256, 640, nc.sync)
+        shift(640, 896, nc.sync)
+        shift(896, 1024, nc.sync)

@@ -17,6 +17,7 @@ P = 128
 PACK = 4
 K, T, S, N, U = 512, 2048, 1024, 128, 1024
 STRIPE = 16
+ROWS = K // 32
 FLOPS = 2 * K * N * S
 
 
@@ -33,27 +34,21 @@ def tile_picked_cbn_silu_p_kernel(tc, x_words, x_scales, w1, gamma, beta, offs, 
 
         offs_sb = sb.tile([P, S // STRIPE], U16)
         cls_sb = sb.tile([P, S // STRIPE], U16)
-        scale_table = sb.tile([P, T], U8, align_bytes=64, tag="scale_then_beta")
         word_table = sb.tile([P, T], I32, align_bytes=64)
-        w_raw = reuse.tile([P, PACK, N], F32, align_bytes=64, offset=0)
         w_grouped = sb.tile([P, N, PACK], BF16, align_bytes=64)
         w_codes = sb.tile([P, N], U32, align_bytes=64)
         w_scales = sb.tile([P, N], U8, align_bytes=64)
         plane = sb.tile([P, S], U8, align_bytes=64)
-        picked_scales = {}
         y = sb.tile([P, S], F32, align_bytes=64)
         scaled = sb.tile([P, S], F32, align_bytes=64)
         shifted = sb.tile([P, S], F32, align_bytes=64)
         result = sb.tile([P, S], F32, align_bytes=64)
         words_in = x_words[0].rearrange("p c t -> p (c t)").bitcast(I32)
+        picked_scales = {}
         picked_words = {}
 
-        def load_scale_rows(u, queue):
-            rows = x_scales[0].bitcast(I32).rearrange("(h u r) c -> u r h c", h=2, u=2)
-            queue.dma_start(scale_table[64 * u + 24 : 64 * u + 32, :].bitcast(I32), rows[u])
-
-        def cast_w(copy):
-            copy(
+        def cast_w():
+            nc.scalar.copy(
                 w_grouped[:].rearrange("p (c i) j -> p c j i", i=4), w_raw[:].rearrange("p j (c i) -> p c j i", i=4)
             )
 
@@ -64,21 +59,18 @@ def tile_picked_cbn_silu_p_kernel(tc, x_words, x_scales, w1, gamma, beta, offs, 
 
         def pick_scales(lo, hi, picked):
             picked_scales[lo] = picked
-            nc.vector.tensor_copy(picked_scales[lo][:], scale_table[:].indirect(entries(offs_sb, lo, hi)))
+            nc.vector.tensor_copy(picked[:], scale_table[:].indirect(entries(offs_sb, lo, hi)))
 
         def place_scales(lo, hi, queue):
-            for h in range(2):
+            for q in range(4):
+                first = P - ROWS + 4 * q
                 queue.dma_start(
-                    plane[64 * h : 64 * h + 64, lo:hi].bitcast(I32), picked_scales[lo][h:P:2, :].bitcast(I32)
+                    plane[32 * q : 32 * q + 4, lo:hi].bitcast(I32), picked_scales[lo][first : first + 4, :].bitcast(I32)
                 )
 
-        def words_tile(base, end, tag):
-            picked_words[base] = sb.tile([P, end - base], U32, align_bytes=64, name="picked_words%d" % base, tag=tag)
-
-        def pick_words(base, lo, hi):
-            nc.vector.tensor_copy(
-                picked_words[base][:, lo - base : hi - base], word_table[:].bitcast(U32).indirect(entries(offs_sb, lo, hi))
-            )
+        def pick_words(lo, hi, picked):
+            picked_words[lo] = picked
+            nc.vector.tensor_copy(picked[:], word_table[:].bitcast(U32).indirect(entries(offs_sb, lo, hi)))
 
         def product(base, lo, hi):
             acc = psum.tile([P, hi - lo], F32, name="acc%d" % lo)
@@ -87,7 +79,7 @@ def tile_picked_cbn_silu_p_kernel(tc, x_words, x_scales, w1, gamma, beta, offs, 
                 lhsT=w_codes[:].bitcast(FP8X4),
                 lhsT_scale=w_scales[:],
                 rhs=picked_words[base][:, lo - base : hi - base].bitcast(FP8X4),
-                rhs_scale=plane[12:P, lo:hi],
+                rhs_scale=plane[:, lo:hi],
                 start=True,
                 stop=True,
             )
@@ -101,37 +93,35 @@ def tile_picked_cbn_silu_p_kernel(tc, x_words, x_scales, w1, gamma, beta, offs, 
             nc.scalar.activation(result[:, lo:hi], shifted[:, lo:hi], SILU)
             queue.dma_start(out[:, lo:hi], result[:, lo:hi])
 
+        scale_table = sb.tile([P, T], U8, align_bytes=64, tag="scale_then_beta")
+        w_raw = reuse.tile([P, PACK, N], F32, align_bytes=64, offset=0)
+        nc.sync.dma_start(scale_table[P - ROWS : P, :].bitcast(I32), x_scales[0].bitcast(I32))
         nc.sync.dma_start(offs_sb[:], offs)
-        load_scale_rows(0, nc.sync)
-        load_scale_rows(1, nc.sync)
-        nc.vector.memset(scale_table[0:24, :].bitcast(I32), 0)
-        nc.gpsimd.memset(scale_table[32:64, :].bitcast(I32), 0)
-        nc.vector.memset(scale_table[64:88, :].bitcast(I32), 0)
-        nc.gpsimd.memset(scale_table[96:P, :].bitcast(I32), 0)
+        nc.vector.memset(scale_table[0 : P - ROWS, :].bitcast(I32), 0)
         nc.sync.dma_start(w_raw[:], w1.rearrange("(p j) m -> p j m", j=PACK))
         nc.sync.dma_start(word_table[:], words_in)
         nc.sync.dma_start(cls_sb[:], cls)
-        cast_w(nc.scalar.copy)
-        gamma_sb = reuse.tile([P, U], F32, align_bytes=64, offset=1024)
-        nc.sync.dma_start(gamma_sb[:], gamma)
+        cast_w()
         first_scales = sb.tile([P, 640], U8, align_bytes=64)
         pick_scales(0, 640, first_scales)
         place_scales(0, 640, nc.sync)
+        gamma_sb = reuse.tile([P, U], F32, align_bytes=64, offset=1024)
+        nc.sync.dma_start(gamma_sb[:], gamma)
         second_scales = reuse.tile([P, S - 640], U8, align_bytes=64, offset=0)
         pick_scales(640, S, second_scales)
         place_scales(640, S, nc.sync)
         quantise_w()
         beta_sb = sb.tile([P, U], F32, align_bytes=64, tag="scale_then_beta")
         nc.sync.dma_start(beta_sb[:], beta)
-        words_tile(0, 256, "a")
-        pick_words(0, 0, 256)
+        words_a = sb.tile([P, 256], U32, align_bytes=64)
+        pick_words(0, 256, words_a)
         product(0, 0, 256)
-        words_tile(256, 640, "b")
-        pick_words(256, 256, 640)
+        words_b = sb.tile([P, 384], U32, align_bytes=64)
+        pick_words(256, 640, words_b)
         product(256, 256, 512)
         product(256, 512, 640)
-        words_tile(640, 1024, "c")
-        pick_words(640, 640, 1024)
+        words_c = sb.tile([P, 384], U32, align_bytes=64)
+        pick_words(640, 1024, words_c)
         product(640, 640, 896)
         product(640, 896, 1024)
         scale(0, 256)

@@ -17,8 +17,17 @@ P = 128
 PACK = 4
 K, T, S, N, U = 512, 2048, 1024, 128, 1024
 STRIPE = 16
-ROWS = K // 32
+BLOCKS = K // 32
+QUADRANT = 32
+ROWS = BLOCKS * QUADRANT // P
+LINE = 4
 FLOPS = 2 * K * N * S
+
+FIRST = 640
+WIDE = 256
+PIECES = ((0, WIDE), (WIDE, FIRST), (FIRST, S))
+STORE_BORDERS = (0, 448, 736, 928, S)
+GAMMA_OFFSET = 1024
 
 
 def entries(offsets, lo, hi):
@@ -37,97 +46,75 @@ def tile_picked_cbn_silu_p_kernel(tc, x_words, x_scales, w1, gamma, beta, offs, 
         word_table = sb.tile([P, T], I32, align_bytes=64)
         w_grouped = sb.tile([P, N, PACK], BF16, align_bytes=64)
         w_codes = sb.tile([P, N], U32, align_bytes=64)
-        w_scales = sb.tile([P, N], U8, align_bytes=64)
-        plane = sb.tile([P, S], U8, align_bytes=64)
+        w_plane = sb.tile([P, N], U8, align_bytes=64)
+        x_plane = sb.tile([P, S], U8, align_bytes=64)
         y = sb.tile([P, S], F32, align_bytes=64)
         scaled = sb.tile([P, S], F32, align_bytes=64)
         shifted = sb.tile([P, S], F32, align_bytes=64)
         result = sb.tile([P, S], F32, align_bytes=64)
-        words_in = x_words[0].rearrange("p c t -> p (c t)").bitcast(I32)
-        picked_scales = {}
-        picked_words = {}
+        scale_table = sb.tile([P, T], U8, align_bytes=64, tag="scale_then_beta")
+        w_raw = reuse.tile([P, PACK, N], F32, align_bytes=64, offset=0)
 
-        def cast_w():
-            nc.scalar.copy(
-                w_grouped[:].rearrange("p (c i) j -> p c j i", i=4), w_raw[:].rearrange("p j (c i) -> p c j i", i=4)
-            )
-
-        def quantise_w():
-            nc.vector.quantize_mx(
-                out=w_codes[:].bitcast(FP8X4), scales=w_scales[:], in_=w_grouped[:].rearrange("p m j -> p (m j)")
-            )
-
-        def pick_scales(lo, hi, picked):
-            picked_scales[lo] = picked
+        def pick_and_place_scales(lo, hi, picked):
             nc.vector.tensor_copy(picked[:], scale_table[:].indirect(entries(offs_sb, lo, hi)))
-
-        def place_scales(lo, hi, queue):
-            for q in range(4):
-                first = P - ROWS + 4 * q
-                queue.dma_start(
-                    plane[32 * q : 32 * q + 4, lo:hi].bitcast(I32), picked_scales[lo][first : first + 4, :].bitcast(I32)
+            for q in range(P // QUADRANT):
+                first = P - BLOCKS + ROWS * q
+                nc.sync.dma_start(
+                    x_plane[QUADRANT * q : QUADRANT * q + ROWS, lo:hi].bitcast(I32),
+                    picked[first : first + ROWS, :].bitcast(I32),
                 )
 
-        def pick_words(lo, hi, picked):
-            picked_words[lo] = picked
-            nc.vector.tensor_copy(picked[:], word_table[:].bitcast(U32).indirect(entries(offs_sb, lo, hi)))
-
-        def product(base, lo, hi):
-            acc = psum.tile([P, hi - lo], F32, name="acc%d" % lo)
-            nc.tensor.matmul_mx(
-                out=acc[:],
-                lhsT=w_codes[:].bitcast(FP8X4),
-                lhsT_scale=w_scales[:],
-                rhs=picked_words[base][:, lo - base : hi - base].bitcast(FP8X4),
-                rhs_scale=plane[:, lo:hi],
-                start=True,
-                stop=True,
-            )
-            nc.scalar.copy(y[:, lo:hi], acc[:])
+        def pick_words_and_multiply(base, end):
+            picked = sb.tile([P, end - base], U32, align_bytes=64, name="words%d" % base)
+            nc.vector.tensor_copy(picked[:], word_table[:].bitcast(U32).indirect(entries(offs_sb, base, end)))
+            for lo in range(base, end, WIDE):
+                hi = min(lo + WIDE, end)
+                acc = psum.tile([P, hi - lo], F32, name="acc%d" % lo)
+                nc.tensor.matmul_mx(
+                    out=acc[:],
+                    lhsT=w_codes[:].bitcast(FP8X4),
+                    lhsT_scale=w_plane[:],
+                    rhs=picked[:, lo - base : hi - base].bitcast(FP8X4),
+                    rhs_scale=x_plane[:, lo:hi],
+                    start=True,
+                    stop=True,
+                )
+                nc.scalar.copy(y[:, lo:hi], acc[:])
 
         def scale(lo, hi):
             nc.vector.tensor_tensor(scaled[:, lo:hi], gamma_sb[:].indirect(entries(cls_sb, lo, hi)), y[:, lo:hi], MULT)
 
-        def shift(lo, hi, queue):
+        def shift_and_store(lo, hi):
             nc.vector.tensor_tensor(shifted[:, lo:hi], beta_sb[:].indirect(entries(cls_sb, lo, hi)), scaled[:, lo:hi], ADD)
             nc.scalar.activation(result[:, lo:hi], shifted[:, lo:hi], SILU)
-            queue.dma_start(out[:, lo:hi], result[:, lo:hi])
+            nc.sync.dma_start(out[:, lo:hi], result[:, lo:hi])
 
-        scale_table = sb.tile([P, T], U8, align_bytes=64, tag="scale_then_beta")
-        w_raw = reuse.tile([P, PACK, N], F32, align_bytes=64, offset=0)
-        nc.sync.dma_start(scale_table[P - ROWS : P, :].bitcast(I32), x_scales[0].bitcast(I32))
+        nc.sync.dma_start(scale_table[P - BLOCKS : P, :].bitcast(I32), x_scales[0].bitcast(I32))
         nc.sync.dma_start(offs_sb[:], offs)
-        nc.vector.memset(scale_table[0 : P - ROWS, :].bitcast(I32), 0)
+        nc.vector.memset(scale_table[0 : P - BLOCKS, :].bitcast(I32), 0)
         nc.sync.dma_start(w_raw[:], w1.rearrange("(p j) m -> p j m", j=PACK))
-        nc.sync.dma_start(word_table[:], words_in)
+        nc.sync.dma_start(word_table[:], x_words[0].rearrange("p c t -> p (c t)").bitcast(I32))
         nc.sync.dma_start(cls_sb[:], cls)
-        cast_w()
-        first_scales = sb.tile([P, 640], U8, align_bytes=64)
-        pick_scales(0, 640, first_scales)
-        place_scales(0, 640, nc.sync)
-        gamma_sb = reuse.tile([P, U], F32, align_bytes=64, offset=1024)
+
+        nc.scalar.copy(
+            w_grouped[:].rearrange("p (c i) j -> p c j i", i=LINE), w_raw[:].rearrange("p j (c i) -> p c j i", i=LINE)
+        )
+
+        first_scales = sb.tile([P, FIRST], U8, align_bytes=64)
+        pick_and_place_scales(0, FIRST, first_scales)
+        gamma_sb = reuse.tile([P, U], F32, align_bytes=64, offset=GAMMA_OFFSET)
         nc.sync.dma_start(gamma_sb[:], gamma)
-        second_scales = reuse.tile([P, S - 640], U8, align_bytes=64, offset=0)
-        pick_scales(640, S, second_scales)
-        place_scales(640, S, nc.sync)
-        quantise_w()
+        second_scales = reuse.tile([P, S - FIRST], U8, align_bytes=64, offset=0)
+        pick_and_place_scales(FIRST, S, second_scales)
+        nc.vector.quantize_mx(
+            out=w_codes[:].bitcast(FP8X4), scales=w_plane[:], in_=w_grouped[:].rearrange("p m j -> p (m j)")
+        )
         beta_sb = sb.tile([P, U], F32, align_bytes=64, tag="scale_then_beta")
         nc.sync.dma_start(beta_sb[:], beta)
-        words_a = sb.tile([P, 256], U32, align_bytes=64)
-        pick_words(0, 256, words_a)
-        product(0, 0, 256)
-        words_b = sb.tile([P, 384], U32, align_bytes=64)
-        pick_words(256, 640, words_b)
-        product(256, 256, 512)
-        product(256, 512, 640)
-        words_c = sb.tile([P, 384], U32, align_bytes=64)
-        pick_words(640, 1024, words_c)
-        product(640, 640, 896)
-        product(640, 896, 1024)
-        scale(0, 256)
-        scale(256, 640)
-        shift(0, 256, nc.sync)
-        scale(640, 1024)
-        shift(256, 640, nc.sync)
-        shift(640, 896, nc.sync)
-        shift(896, 1024, nc.sync)
+
+        for base, end in PIECES:
+            pick_words_and_multiply(base, end)
+        for base, end in PIECES:
+            scale(base, end)
+        for lo, hi in zip(STORE_BORDERS[:-1], STORE_BORDERS[1:]):
+            shift_and_store(lo, hi)

@@ -23,15 +23,19 @@ ROWS = BLOCKS * QUADRANT // P
 LINE = 4
 FLOPS = 2 * K * N * S
 
-FIRST = 640
-WIDE = 256
-PIECES = ((0, WIDE), (WIDE, FIRST), (FIRST, S))
-STORE_BORDERS = (0, 448, 736, 928, S)
-GAMMA_OFFSET = 1024
+SCALE_BORDERS = (0, 384, 1024)
+WORD_BORDERS = (0, 384, 704, 1024)
+PRODUCT_BORDERS = (0, 256, 384, 640, 704, 960, 1024)
+MULT_BORDERS = (0, 384, 704, 1024)
+STORE_BORDERS = (0, 448, 736, 928, 1024)
 
 
 def entries(offsets, lo, hi):
     return offsets[:, lo // STRIPE : hi // STRIPE]
+
+
+def pieces(borders):
+    return list(zip(borders[:-1], borders[1:]))
 
 
 def tile_picked_cbn_silu_p_kernel(tc, x_words, x_scales, w1, gamma, beta, offs, cls, out):
@@ -47,47 +51,24 @@ def tile_picked_cbn_silu_p_kernel(tc, x_words, x_scales, w1, gamma, beta, offs, 
         w_grouped = sb.tile([P, N, PACK], BF16, align_bytes=64)
         w_codes = sb.tile([P, N], U32, align_bytes=64)
         w_plane = sb.tile([P, N], U8, align_bytes=64)
-        x_plane = sb.tile([P, S], U8, align_bytes=64)
         y = sb.tile([P, S], F32, align_bytes=64)
         scaled = sb.tile([P, S], F32, align_bytes=64)
         shifted = sb.tile([P, S], F32, align_bytes=64)
         result = sb.tile([P, S], F32, align_bytes=64)
+
         scale_table = sb.tile([P, T], U8, align_bytes=64, tag="scale_then_beta")
         w_raw = reuse.tile([P, PACK, N], F32, align_bytes=64, offset=0)
+        first = SCALE_BORDERS[1]
 
-        def pick_and_place_scales(lo, hi, picked):
+        def pick_and_place_scales(lo, hi, plane, queues):
+            picked = sb.tile([P, hi - lo], U8, align_bytes=64, name="scales%d" % lo)
             nc.vector.tensor_copy(picked[:], scale_table[:].indirect(entries(offs_sb, lo, hi)))
             for q in range(P // QUADRANT):
-                first = P - BLOCKS + ROWS * q
-                nc.sync.dma_start(
-                    x_plane[QUADRANT * q : QUADRANT * q + ROWS, lo:hi].bitcast(I32),
-                    picked[first : first + ROWS, :].bitcast(I32),
+                row = P - BLOCKS + ROWS * q
+                queues[q].dma_start(
+                    plane[QUADRANT * q : QUADRANT * q + ROWS, :].bitcast(I32),
+                    picked[row : row + ROWS, :].bitcast(I32),
                 )
-
-        def pick_words_and_multiply(base, end):
-            picked = sb.tile([P, end - base], U32, align_bytes=64, name="words%d" % base)
-            nc.vector.tensor_copy(picked[:], word_table[:].bitcast(U32).indirect(entries(offs_sb, base, end)))
-            for lo in range(base, end, WIDE):
-                hi = min(lo + WIDE, end)
-                acc = psum.tile([P, hi - lo], F32, name="acc%d" % lo)
-                nc.tensor.matmul_mx(
-                    out=acc[:],
-                    lhsT=w_codes[:].bitcast(FP8X4),
-                    lhsT_scale=w_plane[:],
-                    rhs=picked[:, lo - base : hi - base].bitcast(FP8X4),
-                    rhs_scale=x_plane[:, lo:hi],
-                    start=True,
-                    stop=True,
-                )
-                nc.scalar.copy(y[:, lo:hi], acc[:])
-
-        def scale(lo, hi):
-            nc.vector.tensor_tensor(scaled[:, lo:hi], gamma_sb[:].indirect(entries(cls_sb, lo, hi)), y[:, lo:hi], MULT)
-
-        def shift_and_store(lo, hi):
-            nc.vector.tensor_tensor(shifted[:, lo:hi], beta_sb[:].indirect(entries(cls_sb, lo, hi)), scaled[:, lo:hi], ADD)
-            nc.scalar.activation(result[:, lo:hi], shifted[:, lo:hi], SILU)
-            nc.sync.dma_start(out[:, lo:hi], result[:, lo:hi])
 
         nc.sync.dma_start(scale_table[P - BLOCKS : P, :].bitcast(I32), x_scales[0].bitcast(I32))
         nc.sync.dma_start(offs_sb[:], offs)
@@ -99,22 +80,37 @@ def tile_picked_cbn_silu_p_kernel(tc, x_words, x_scales, w1, gamma, beta, offs, 
         nc.scalar.copy(
             w_grouped[:].rearrange("p (c i) j -> p c j i", i=LINE), w_raw[:].rearrange("p j (c i) -> p c j i", i=LINE)
         )
-
-        first_scales = sb.tile([P, FIRST], U8, align_bytes=64)
-        pick_and_place_scales(0, FIRST, first_scales)
-        gamma_sb = reuse.tile([P, U], F32, align_bytes=64, offset=GAMMA_OFFSET)
+        first_plane = sb.tile([P, first], U8, align_bytes=64)
+        pick_and_place_scales(0, first, first_plane, [nc.sync] * 4)
+        gamma_sb = reuse.tile([P, U], F32, align_bytes=64, offset=1024)
         nc.sync.dma_start(gamma_sb[:], gamma)
-        second_scales = reuse.tile([P, S - FIRST], U8, align_bytes=64, offset=0)
-        pick_and_place_scales(FIRST, S, second_scales)
+        second_plane = reuse.tile([P, S - first], U8, align_bytes=64, offset=0)
+        pick_and_place_scales(first, S, second_plane, [nc.sync] * 4)
         nc.vector.quantize_mx(
             out=w_codes[:].bitcast(FP8X4), scales=w_plane[:], in_=w_grouped[:].rearrange("p m j -> p (m j)")
         )
         beta_sb = sb.tile([P, U], F32, align_bytes=64, tag="scale_then_beta")
         nc.sync.dma_start(beta_sb[:], beta)
 
-        for base, end in PIECES:
-            pick_words_and_multiply(base, end)
-        for base, end in PIECES:
-            scale(base, end)
-        for lo, hi in zip(STORE_BORDERS[:-1], STORE_BORDERS[1:]):
-            shift_and_store(lo, hi)
+        for base, end in pieces(WORD_BORDERS):
+            picked = sb.tile([P, end - base], U32, align_bytes=64, name="words%d" % base)
+            nc.vector.tensor_copy(picked[:], word_table[:].bitcast(U32).indirect(entries(offs_sb, base, end)))
+            for lo, hi in pieces(PRODUCT_BORDERS):
+                if base <= lo < end:
+                    acc = psum.tile([P, hi - lo], F32, name="acc%d" % lo)
+                    nc.tensor.matmul_mx(
+                        out=acc[:],
+                        lhsT=w_codes[:].bitcast(FP8X4),
+                        lhsT_scale=w_plane[:],
+                        rhs=picked[:, lo - base : hi - base].bitcast(FP8X4),
+                        rhs_scale=first_plane[:, lo:hi] if lo < first else second_plane[:, lo - first : hi - first],
+                        start=True,
+                        stop=True,
+                    )
+                    nc.scalar.copy(y[:, lo:hi], acc[:])
+        for lo, hi in pieces(MULT_BORDERS):
+            nc.vector.tensor_tensor(scaled[:, lo:hi], gamma_sb[:].indirect(entries(cls_sb, lo, hi)), y[:, lo:hi], MULT)
+        for lo, hi in pieces(STORE_BORDERS):
+            nc.vector.tensor_tensor(shifted[:, lo:hi], beta_sb[:].indirect(entries(cls_sb, lo, hi)), scaled[:, lo:hi], ADD)
+            nc.scalar.activation(result[:, lo:hi], shifted[:, lo:hi], SILU)
+            nc.sync.dma_start(out[:, lo:hi], result[:, lo:hi])

@@ -27,7 +27,7 @@ SCALE_BORDERS = (0, 384, 1024)
 WORD_BORDERS = (0, 384, 704, 1024)
 PRODUCT_BORDERS = (0, 256, 384, 640, 704, 960, 1024)
 MULT_BORDERS = (0, 384, 704, 1024)
-STORE_BORDERS = (0, 448, 736, 928, 1024)
+STORE_BORDERS = (0, 352, 640, 864, 1024)
 
 
 def entries(offsets, lo, hi):

@@ -11,6 +11,7 @@ U8 = mybir.dt.uint8
 FP8X4 = mybir.dt.float8_e4m3fn_x4
 MULT = mybir.AluOpType.mult
 ADD = mybir.AluOpType.add
+COPY = mybir.ActivationFunctionType.Copy
 SILU = mybir.ActivationFunctionType.Silu
 
 P = 128
@@ -23,10 +24,7 @@ ROWS = BLOCKS * QUADRANT // P
 LINE = 4
 FLOPS = 2 * K * N * S
 
-SCALE_BORDERS = (0, 384, 1024)
-WORD_BORDERS = (0, 384, 704, 1024)
-PRODUCT_BORDERS = (0, 256, 384, 640, 704, 960, 1024)
-MULT_BORDERS = (0, 384, 704, 1024)
+HALVES = (0, 512, 1024)
 STORE_BORDERS = (0, 352, 640, 864, 1024)
 
 
@@ -42,75 +40,76 @@ def tile_picked_cbn_silu_p_kernel(tc, x_words, x_scales, w1, gamma, beta, offs, 
     nc = tc.nc
     with ExitStack() as ctx:
         sb = ctx.enter_context(tc.tile_pool(name="sb", bufs=1))
-        reuse = ctx.enter_context(tc.tile_pool(name="reuse", bufs=1))
         psum = ctx.enter_context(tc.psum_pool(name="psum", bufs=1))
 
         offs_sb = sb.tile([P, S // STRIPE], U16)
         cls_sb = sb.tile([P, S // STRIPE], U16)
+        scale_table = sb.tile([P, T], U8, align_bytes=64)
         word_table = sb.tile([P, T], I32, align_bytes=64)
+        gamma_sb = sb.tile([P, U], F32, align_bytes=64)
+        beta_sb = sb.tile([P, U], F32, align_bytes=64)
+        w_raw = sb.tile([P, PACK, N], F32, align_bytes=64)
         w_grouped = sb.tile([P, N, PACK], BF16, align_bytes=64)
         w_codes = sb.tile([P, N], U32, align_bytes=64)
         w_plane = sb.tile([P, N], U8, align_bytes=64)
-        y = sb.tile([P, S], F32, align_bytes=64)
+        picked_scales = sb.tile([P, S], U8, align_bytes=64)
+        x_plane = sb.tile([P, S], U8, align_bytes=64)
+        gain = sb.tile([P, S], F32, align_bytes=64)
+        shift = sb.tile([P, S], F32, align_bytes=64)
         scaled = sb.tile([P, S], F32, align_bytes=64)
         shifted = sb.tile([P, S], F32, align_bytes=64)
         result = sb.tile([P, S], F32, align_bytes=64)
+        warm = sb.tile([P, 2], F32, align_bytes=64)
 
-        scale_table = sb.tile([P, T], U8, align_bytes=64, tag="scale_then_beta")
-        w_raw = reuse.tile([P, PACK, N], F32, align_bytes=64, offset=0)
-        first = SCALE_BORDERS[1]
-
-        def pick_and_place_scales(lo, hi, plane, queues):
-            picked = sb.tile([P, hi - lo], U8, align_bytes=64, name="scales%d" % lo)
-            nc.vector.tensor_copy(picked[:], scale_table[:].indirect(entries(offs_sb, lo, hi)))
-            for q in range(P // QUADRANT):
-                row = P - BLOCKS + ROWS * q
-                queues[q].dma_start(
-                    plane[QUADRANT * q : QUADRANT * q + ROWS, :].bitcast(I32),
-                    picked[row : row + ROWS, :].bitcast(I32),
-                )
+        nc.gpsimd.memset(warm[:, 0:1], 0.0)
+        nc.scalar.activation(warm[:, 1:2], warm[:, 0:1], SILU)
 
         nc.sync.dma_start(scale_table[P - BLOCKS : P, :].bitcast(I32), x_scales[0].bitcast(I32))
         nc.sync.dma_start(offs_sb[:], offs)
         nc.vector.memset(scale_table[0 : P - BLOCKS, :].bitcast(I32), 0)
         nc.sync.dma_start(w_raw[:], w1.rearrange("(p j) m -> p j m", j=PACK))
-        nc.sync.dma_start(word_table[:], x_words[0].rearrange("p c t -> p (c t)").bitcast(I32))
         nc.sync.dma_start(cls_sb[:], cls)
+        nc.sync.dma_start(gamma_sb[:], gamma)
+        nc.sync.dma_start(word_table[:], x_words[0].rearrange("p c t -> p (c t)").bitcast(I32))
+        nc.sync.dma_start(beta_sb[:], beta)
+
+        nc.vector.tensor_copy(picked_scales[:], scale_table[:].indirect(offs_sb[:]))
+        for q in range(P // QUADRANT):
+            row = P - BLOCKS + ROWS * q
+            nc.sync.dma_start(
+                x_plane[QUADRANT * q : QUADRANT * q + ROWS, :].bitcast(I32),
+                picked_scales[row : row + ROWS, :].bitcast(I32),
+            )
 
         nc.scalar.copy(
             w_grouped[:].rearrange("p (c i) j -> p c j i", i=LINE), w_raw[:].rearrange("p j (c i) -> p c j i", i=LINE)
         )
-        first_plane = sb.tile([P, first], U8, align_bytes=64)
-        pick_and_place_scales(0, first, first_plane, [nc.sync] * 4)
-        gamma_sb = reuse.tile([P, U], F32, align_bytes=64, offset=1024)
-        nc.sync.dma_start(gamma_sb[:], gamma)
-        second_plane = reuse.tile([P, S - first], U8, align_bytes=64, offset=0)
-        pick_and_place_scales(first, S, second_plane, [nc.sync] * 4)
         nc.vector.quantize_mx(
             out=w_codes[:].bitcast(FP8X4), scales=w_plane[:], in_=w_grouped[:].rearrange("p m j -> p (m j)")
         )
-        beta_sb = sb.tile([P, U], F32, align_bytes=64, tag="scale_then_beta")
-        nc.sync.dma_start(beta_sb[:], beta)
+        for lo, hi in pieces(HALVES):
+            nc.scalar.activation(gain[:, lo:hi], gamma_sb[:].indirect(entries(cls_sb, lo, hi)), COPY)
 
-        for base, end in pieces(WORD_BORDERS):
-            picked = sb.tile([P, end - base], U32, align_bytes=64, name="words%d" % base)
-            nc.vector.tensor_copy(picked[:], word_table[:].bitcast(U32).indirect(entries(offs_sb, base, end)))
-            for lo, hi in pieces(PRODUCT_BORDERS):
-                if base <= lo < end:
-                    acc = psum.tile([P, hi - lo], F32, name="acc%d" % lo)
-                    nc.tensor.matmul_mx(
-                        out=acc[:],
-                        lhsT=w_codes[:].bitcast(FP8X4),
-                        lhsT_scale=w_plane[:],
-                        rhs=picked[:, lo - base : hi - base].bitcast(FP8X4),
-                        rhs_scale=first_plane[:, lo:hi] if lo < first else second_plane[:, lo - first : hi - first],
-                        start=True,
-                        stop=True,
-                    )
-                    nc.scalar.copy(y[:, lo:hi], acc[:])
-        for lo, hi in pieces(MULT_BORDERS):
-            nc.vector.tensor_tensor(scaled[:, lo:hi], gamma_sb[:].indirect(entries(cls_sb, lo, hi)), y[:, lo:hi], MULT)
+        sums = []
+        for lo, hi in pieces(HALVES):
+            picked = sb.tile([P, hi - lo], U32, align_bytes=64, name="words%d" % lo)
+            nc.vector.tensor_copy(picked[:], word_table[:].bitcast(U32).indirect(entries(offs_sb, lo, hi)))
+            acc = psum.tile([P, hi - lo], F32, name="acc%d" % lo)
+            nc.tensor.matmul_mx(
+                out=acc[:],
+                lhsT=w_codes[:].bitcast(FP8X4),
+                lhsT_scale=w_plane[:],
+                rhs=picked[:].bitcast(FP8X4),
+                rhs_scale=x_plane[:, lo:hi],
+                start=True,
+                stop=True,
+            )
+            sums.append(acc)
+        for lo, hi in pieces(HALVES):
+            nc.scalar.activation(shift[:, lo:hi], beta_sb[:].indirect(entries(cls_sb, lo, hi)), COPY)
+        for acc, (lo, hi) in zip(sums, pieces(HALVES)):
+            nc.vector.tensor_tensor(scaled[:, lo:hi], acc[:], gain[:, lo:hi], MULT)
         for lo, hi in pieces(STORE_BORDERS):
-            nc.vector.tensor_tensor(shifted[:, lo:hi], beta_sb[:].indirect(entries(cls_sb, lo, hi)), scaled[:, lo:hi], ADD)
+            nc.vector.tensor_tensor(shifted[:, lo:hi], scaled[:, lo:hi], shift[:, lo:hi], ADD)
             nc.scalar.activation(result[:, lo:hi], shifted[:, lo:hi], SILU)
             nc.sync.dma_start(out[:, lo:hi], result[:, lo:hi])

@@ -24,8 +24,8 @@ ROWS = BLOCKS * QUADRANT // P
 LINE = 4
 FLOPS = 2 * K * N * S
 
-HALVES = (0, 512, 1024)
-STORE_BORDERS = (0, 352, 640, 864, 1024)
+HALF = S // 2
+QUARTER = S // 4
 
 
 def entries(offsets, lo, hi):
@@ -40,6 +40,8 @@ def tile_picked_cbn_silu_p_kernel(tc, x_words, x_scales, w1, gamma, beta, offs, 
     nc = tc.nc
     with ExitStack() as ctx:
         sb = ctx.enter_context(tc.tile_pool(name="sb", bufs=1))
+        reuse = ctx.enter_context(tc.tile_pool(name="reuse", bufs=1))
+        ring = ctx.enter_context(tc.tile_pool(name="ring", bufs=2))
         psum = ctx.enter_context(tc.psum_pool(name="psum", bufs=1))
 
         offs_sb = sb.tile([P, S // STRIPE], U16)
@@ -47,19 +49,25 @@ def tile_picked_cbn_silu_p_kernel(tc, x_words, x_scales, w1, gamma, beta, offs, 
         scale_table = sb.tile([P, T], U8, align_bytes=64)
         word_table = sb.tile([P, T], I32, align_bytes=64)
         gamma_sb = sb.tile([P, U], F32, align_bytes=64)
-        beta_sb = sb.tile([P, U], F32, align_bytes=64)
-        w_raw = sb.tile([P, PACK, N], F32, align_bytes=64)
         w_grouped = sb.tile([P, N, PACK], BF16, align_bytes=64)
         w_codes = sb.tile([P, N], U32, align_bytes=64)
         w_plane = sb.tile([P, N], U8, align_bytes=64)
-        picked_scales = sb.tile([P, S], U8, align_bytes=64)
-        x_plane = sb.tile([P, S], U8, align_bytes=64)
         gain = sb.tile([P, S], F32, align_bytes=64)
-        shift = sb.tile([P, S], F32, align_bytes=64)
-        scaled = sb.tile([P, S], F32, align_bytes=64)
+        shift = sb.tile([P, QUARTER], F32, align_bytes=64)
         shifted = sb.tile([P, S], F32, align_bytes=64)
         result = sb.tile([P, S], F32, align_bytes=64)
         warm = sb.tile([P, 2], F32, align_bytes=64)
+        w_raw = reuse.tile([P, PACK, N], F32, align_bytes=64, offset=0)
+
+        def pick_and_place_scales(lo, plane):
+            picked = sb.tile([P, HALF], U8, align_bytes=64, name="scales%d" % lo)
+            nc.vector.tensor_copy(picked[:], scale_table[:].indirect(entries(offs_sb, lo, lo + HALF)))
+            for q in range(P // QUADRANT):
+                row = P - BLOCKS + ROWS * q
+                nc.sync.dma_start(
+                    plane[QUADRANT * q : QUADRANT * q + ROWS, :].bitcast(I32),
+                    picked[row : row + ROWS, :].bitcast(I32),
+                )
 
         nc.gpsimd.memset(warm[:, 0:1], 0.0)
         nc.scalar.activation(warm[:, 1:2], warm[:, 0:1], SILU)
@@ -68,48 +76,51 @@ def tile_picked_cbn_silu_p_kernel(tc, x_words, x_scales, w1, gamma, beta, offs, 
         nc.sync.dma_start(offs_sb[:], offs)
         nc.vector.memset(scale_table[0 : P - BLOCKS, :].bitcast(I32), 0)
         nc.sync.dma_start(w_raw[:], w1.rearrange("(p j) m -> p j m", j=PACK))
+        nc.sync.dma_start(word_table[:], x_words[0].rearrange("p c t -> p (c t)").bitcast(I32))
         nc.sync.dma_start(cls_sb[:], cls)
         nc.sync.dma_start(gamma_sb[:], gamma)
-        nc.sync.dma_start(word_table[:], x_words[0].rearrange("p c t -> p (c t)").bitcast(I32))
-        nc.sync.dma_start(beta_sb[:], beta)
-
-        nc.vector.tensor_copy(picked_scales[:], scale_table[:].indirect(offs_sb[:]))
-        for q in range(P // QUADRANT):
-            row = P - BLOCKS + ROWS * q
-            nc.sync.dma_start(
-                x_plane[QUADRANT * q : QUADRANT * q + ROWS, :].bitcast(I32),
-                picked_scales[row : row + ROWS, :].bitcast(I32),
-            )
 
         nc.scalar.copy(
             w_grouped[:].rearrange("p (c i) j -> p c j i", i=LINE), w_raw[:].rearrange("p j (c i) -> p c j i", i=LINE)
         )
+        first_plane = sb.tile([P, HALF], U8, align_bytes=64)
+        pick_and_place_scales(0, first_plane)
+        beta_sb = reuse.tile([P, U], F32, align_bytes=64, offset=1024)
+        nc.sync.dma_start(beta_sb[:], beta)
+        second_plane = reuse.tile([P, HALF], U8, align_bytes=64, offset=0)
+        pick_and_place_scales(HALF, second_plane)
         nc.vector.quantize_mx(
             out=w_codes[:].bitcast(FP8X4), scales=w_plane[:], in_=w_grouped[:].rearrange("p m j -> p (m j)")
         )
-        for lo, hi in pieces(HALVES):
-            nc.scalar.activation(gain[:, lo:hi], gamma_sb[:].indirect(entries(cls_sb, lo, hi)), COPY)
 
         sums = []
-        for lo, hi in pieces(HALVES):
-            picked = sb.tile([P, hi - lo], U32, align_bytes=64, name="words%d" % lo)
-            nc.vector.tensor_copy(picked[:], word_table[:].bitcast(U32).indirect(entries(offs_sb, lo, hi)))
-            acc = psum.tile([P, hi - lo], F32, name="acc%d" % lo)
-            nc.tensor.matmul_mx(
-                out=acc[:],
-                lhsT=w_codes[:].bitcast(FP8X4),
-                lhsT_scale=w_plane[:],
-                rhs=picked[:].bitcast(FP8X4),
-                rhs_scale=x_plane[:, lo:hi],
-                start=True,
-                stop=True,
-            )
-            sums.append(acc)
-        for lo, hi in pieces(HALVES):
-            nc.scalar.activation(shift[:, lo:hi], beta_sb[:].indirect(entries(cls_sb, lo, hi)), COPY)
-        for acc, (lo, hi) in zip(sums, pieces(HALVES)):
-            nc.vector.tensor_tensor(scaled[:, lo:hi], acc[:], gain[:, lo:hi], MULT)
-        for lo, hi in pieces(STORE_BORDERS):
-            nc.vector.tensor_tensor(shifted[:, lo:hi], scaled[:, lo:hi], shift[:, lo:hi], ADD)
-            nc.scalar.activation(result[:, lo:hi], shifted[:, lo:hi], SILU)
-            nc.sync.dma_start(out[:, lo:hi], result[:, lo:hi])
+        for base, plane in ((0, first_plane), (HALF, second_plane)):
+            picked = sb.tile([P, HALF], U32, align_bytes=64, name="words%d" % base)
+            nc.vector.tensor_copy(picked[:], word_table[:].bitcast(U32).indirect(entries(offs_sb, base, base + HALF)))
+            for lo in (0, QUARTER):
+                acc = psum.tile([P, QUARTER], F32, name="acc%d" % (base + lo))
+                nc.tensor.matmul_mx(
+                    out=acc[:],
+                    lhsT=w_codes[:].bitcast(FP8X4),
+                    lhsT_scale=w_plane[:],
+                    rhs=picked[:, lo : lo + QUARTER].bitcast(FP8X4),
+                    rhs_scale=plane[:, lo : lo + QUARTER],
+                    start=True,
+                    stop=True,
+                )
+                sums.append(acc)
+        for lo in range(0, S, QUARTER):
+            nc.scalar.activation(gain[:, lo : lo + QUARTER], gamma_sb[:].indirect(entries(cls_sb, lo, lo + QUARTER)), COPY)
+        nc.scalar.activation(shift[:], beta_sb[:].indirect(entries(cls_sb, S - QUARTER, S)), COPY)
+
+        for base in (0, HALF):
+            scaled = {}
+            for lo in (base, base + QUARTER):
+                scaled[lo] = ring.tile([P, QUARTER], F32, align_bytes=64, name="scaled")
+                nc.vector.tensor_tensor(scaled[lo][:], sums[lo // QUARTER][:], gain[:, lo : lo + QUARTER], MULT)
+            for lo in (base, base + QUARTER):
+                hi = lo + QUARTER
+                looked_up = shift[:] if hi == S else beta_sb[:].indirect(entries(cls_sb, lo, hi))
+                nc.vector.tensor_tensor(shifted[:, lo:hi], looked_up, scaled[lo][:], ADD)
+                nc.scalar.activation(result[:, lo:hi], shifted[:, lo:hi], SILU)
+                nc.sync.dma_start(out[:, lo:hi], result[:, lo:hi])

@@ -26,6 +26,8 @@ FLOPS = 2 * K * N * S
 
 HALF = S // 2
 QUARTER = S // 4
+LAST = 832
+GAIN_BORDERS = (0, QUARTER, HALF, S)
 
 
 def entries(offsets, lo, hi):
@@ -53,7 +55,7 @@ def tile_picked_cbn_silu_p_kernel(tc, x_words, x_scales, w1, gamma, beta, offs, 
         w_codes = sb.tile([P, N], U32, align_bytes=64)
         w_plane = sb.tile([P, N], U8, align_bytes=64)
         gain = sb.tile([P, S], F32, align_bytes=64)
-        shift = sb.tile([P, QUARTER], F32, align_bytes=64)
+        shift = sb.tile([P, LAST - HALF], F32, align_bytes=64)
         shifted = sb.tile([P, S], F32, align_bytes=64)
         result = sb.tile([P, S], F32, align_bytes=64)
         warm = sb.tile([P, 2], F32, align_bytes=64)
@@ -93,14 +95,14 @@ def tile_picked_cbn_silu_p_kernel(tc, x_words, x_scales, w1, gamma, beta, offs, 
             out=w_codes[:].bitcast(FP8X4), scales=w_plane[:], in_=w_grouped[:].rearrange("p m j -> p (m j)")
         )
 
-        sums = []
+        sums = {}
         for base, plane in ((0, first_plane), (HALF, second_plane)):
             picked = sb.tile([P, HALF], U32, align_bytes=64, name="words%d" % base)
             nc.vector.tensor_copy(picked[:], word_table[:].bitcast(U32).indirect(entries(offs_sb, base, base + HALF)))
+            sums[base] = psum.tile([P, HALF], F32, name="acc%d" % base)
             for lo in (0, QUARTER):
-                acc = psum.tile([P, QUARTER], F32, name="acc%d" % (base + lo))
                 nc.tensor.matmul_mx(
-                    out=acc[:],
+                    out=sums[base][:, lo : lo + QUARTER],
                     lhsT=w_codes[:].bitcast(FP8X4),
                     lhsT_scale=w_plane[:],
                     rhs=picked[:, lo : lo + QUARTER].bitcast(FP8X4),
@@ -108,19 +110,17 @@ def tile_picked_cbn_silu_p_kernel(tc, x_words, x_scales, w1, gamma, beta, offs, 
                     start=True,
                     stop=True,
                 )
-                sums.append(acc)
-        for lo in range(0, S, QUARTER):
-            nc.scalar.activation(gain[:, lo : lo + QUARTER], gamma_sb[:].indirect(entries(cls_sb, lo, lo + QUARTER)), COPY)
-        nc.scalar.activation(shift[:], beta_sb[:].indirect(entries(cls_sb, S - QUARTER, S)), COPY)
+        for lo, hi in pieces(GAIN_BORDERS):
+            nc.scalar.activation(gain[:, lo:hi], gamma_sb[:].indirect(entries(cls_sb, lo, hi)), COPY)
+        nc.scalar.activation(shift[:], beta_sb[:].indirect(entries(cls_sb, HALF, LAST)), COPY)
 
-        for base in (0, HALF):
+        for base, border in ((0, QUARTER), (HALF, LAST)):
             scaled = {}
-            for lo in (base, base + QUARTER):
-                scaled[lo] = ring.tile([P, QUARTER], F32, align_bytes=64, name="scaled")
-                nc.vector.tensor_tensor(scaled[lo][:], sums[lo // QUARTER][:], gain[:, lo : lo + QUARTER], MULT)
-            for lo in (base, base + QUARTER):
-                hi = lo + QUARTER
-                looked_up = shift[:] if hi == S else beta_sb[:].indirect(entries(cls_sb, lo, hi))
+            for lo, hi in pieces((base, border, base + HALF)):
+                scaled[lo] = ring.tile([P, hi - lo], F32, align_bytes=64, name="scaled")
+                nc.vector.tensor_tensor(scaled[lo][:], sums[base][:, lo - base : hi - base], gain[:, lo:hi], MULT)
+            for lo, hi in pieces((base, border, base + HALF)):
+                looked_up = shift[:] if lo == HALF else beta_sb[:].indirect(entries(cls_sb, lo, hi))
                 nc.vector.tensor_tensor(shifted[:, lo:hi], looked_up, scaled[lo][:], ADD)
                 nc.scalar.activation(result[:, lo:hi], shifted[:, lo:hi], SILU)
                 nc.sync.dma_start(out[:, lo:hi], result[:, lo:hi])

@@ -26,8 +26,12 @@ FLOPS = 2 * K * N * S
 
 HALF = S // 2
 QUARTER = S // 4
-LAST = 832
-GAIN_BORDERS = (0, QUARTER, HALF, S)
+LAST = 896
+SUM_BORDERS = (0, 256, 512, 768, 896, 1024)
+EARLY = 640
+PRODUCT_BORDERS = (0, 256, 512, 640, 768, 1024)
+SECOND = 256
+TABLE_AT = 4 * PACK * N
 
 
 def entries(offsets, lo, hi):
@@ -48,7 +52,7 @@ def tile_picked_cbn_silu_p_kernel(tc, x_words, x_scales, w1, gamma, beta, offs, 
 
         offs_sb = sb.tile([P, S // STRIPE], U16)
         cls_sb = sb.tile([P, S // STRIPE], U16)
-        scale_table = sb.tile([P, T], U8, align_bytes=64)
+        scale_table = reuse.tile([P, T], U8, align_bytes=64, offset=TABLE_AT)
         word_table = sb.tile([P, T], I32, align_bytes=64)
         gamma_sb = sb.tile([P, U], F32, align_bytes=64)
         w_grouped = sb.tile([P, N, PACK], BF16, align_bytes=64)
@@ -61,9 +65,12 @@ def tile_picked_cbn_silu_p_kernel(tc, x_words, x_scales, w1, gamma, beta, offs, 
         warm = sb.tile([P, 2], F32, align_bytes=64)
         w_raw = reuse.tile([P, PACK, N], F32, align_bytes=64, offset=0)
 
-        def pick_and_place_scales(lo, plane):
+        def pick_scales(lo):
             picked = sb.tile([P, HALF], U8, align_bytes=64, name="scales%d" % lo)
             nc.vector.tensor_copy(picked[:], scale_table[:].indirect(entries(offs_sb, lo, lo + HALF)))
+            return picked
+
+        def place_scales(picked, plane):
             for q in range(P // QUADRANT):
                 row = P - BLOCKS + ROWS * q
                 nc.sync.dma_start(
@@ -77,8 +84,8 @@ def tile_picked_cbn_silu_p_kernel(tc, x_words, x_scales, w1, gamma, beta, offs, 
         nc.sync.dma_start(scale_table[P - BLOCKS : P, :].bitcast(I32), x_scales[0].bitcast(I32))
         nc.sync.dma_start(offs_sb[:], offs)
         nc.vector.memset(scale_table[0 : P - BLOCKS, :].bitcast(I32), 0)
-        nc.sync.dma_start(w_raw[:], w1.rearrange("(p j) m -> p j m", j=PACK))
         nc.sync.dma_start(word_table[:], x_words[0].rearrange("p c t -> p (c t)").bitcast(I32))
+        nc.sync.dma_start(w_raw[:], w1.rearrange("(p j) m -> p j m", j=PACK))
         nc.sync.dma_start(cls_sb[:], cls)
         nc.sync.dma_start(gamma_sb[:], gamma)
 
@@ -86,41 +93,50 @@ def tile_picked_cbn_silu_p_kernel(tc, x_words, x_scales, w1, gamma, beta, offs, 
             w_grouped[:].rearrange("p (c i) j -> p c j i", i=LINE), w_raw[:].rearrange("p j (c i) -> p c j i", i=LINE)
         )
         first_plane = sb.tile([P, HALF], U8, align_bytes=64)
-        pick_and_place_scales(0, first_plane)
-        beta_sb = reuse.tile([P, U], F32, align_bytes=64, offset=1024)
+        place_scales(pick_scales(0), first_plane)
+        late_scales = pick_scales(HALF)
+        beta_sb = reuse.tile([P, U], F32, align_bytes=64, offset=TABLE_AT + HALF)
         nc.sync.dma_start(beta_sb[:], beta)
-        second_plane = reuse.tile([P, HALF], U8, align_bytes=64, offset=0)
-        pick_and_place_scales(HALF, second_plane)
+        second_plane = reuse.tile([P, HALF], U8, align_bytes=64, offset=TABLE_AT)
+        place_scales(late_scales, second_plane)
         nc.vector.quantize_mx(
             out=w_codes[:].bitcast(FP8X4), scales=w_plane[:], in_=w_grouped[:].rearrange("p m j -> p (m j)")
         )
 
-        sums = {}
-        for base, plane in ((0, first_plane), (HALF, second_plane)):
-            picked = sb.tile([P, HALF], U32, align_bytes=64, name="words%d" % base)
-            nc.vector.tensor_copy(picked[:], word_table[:].bitcast(U32).indirect(entries(offs_sb, base, base + HALF)))
-            sums[base] = psum.tile([P, HALF], F32, name="acc%d" % base)
-            for lo in (0, QUARTER):
-                nc.tensor.matmul_mx(
-                    out=sums[base][:, lo : lo + QUARTER],
-                    lhsT=w_codes[:].bitcast(FP8X4),
-                    lhsT_scale=w_plane[:],
-                    rhs=picked[:, lo : lo + QUARTER].bitcast(FP8X4),
-                    rhs_scale=plane[:, lo : lo + QUARTER],
-                    start=True,
-                    stop=True,
-                )
-        for lo, hi in pieces(GAIN_BORDERS):
+        early_words = sb.tile([P, EARLY], U32, align_bytes=64)
+        nc.vector.tensor_copy(early_words[:], word_table[:].bitcast(U32).indirect(entries(offs_sb, 0, EARLY)))
+        late_words = reuse.tile([P, S - EARLY], U32, align_bytes=64, offset=0)
+        nc.vector.tensor_copy(late_words[:], word_table[:].bitcast(U32).indirect(entries(offs_sb, EARLY, S)))
+        sums = {0: psum.tile([P, HALF], F32, name="first_sums"), HALF: psum.tile([P, HALF], F32, name="second_sums")}
+        for lo, hi in pieces(PRODUCT_BORDERS):
+            base, plane = (0, first_plane) if lo < HALF else (HALF, second_plane)
+            words = early_words[:, lo:hi] if lo < EARLY else late_words[:, lo - EARLY : hi - EARLY]
+            nc.tensor.matmul_mx(
+                out=sums[base][:, lo - base : hi - base],
+                lhsT=w_codes[:].bitcast(FP8X4),
+                lhsT_scale=w_plane[:],
+                rhs=words.bitcast(FP8X4),
+                rhs_scale=plane[:, lo - base : hi - base],
+                start=True,
+                stop=True,
+            )
+        nc.vector.tensor_copy(gain[:, SECOND:HALF], gamma_sb[:].indirect(entries(cls_sb, SECOND, HALF)))
+        for lo, hi in ((0, SECOND), (HALF, S)):
             nc.scalar.activation(gain[:, lo:hi], gamma_sb[:].indirect(entries(cls_sb, lo, hi)), COPY)
         nc.scalar.activation(shift[:], beta_sb[:].indirect(entries(cls_sb, HALF, LAST)), COPY)
 
-        for base, border in ((0, QUARTER), (HALF, LAST)):
+        for base in (0, HALF):
             scaled = {}
-            for lo, hi in pieces((base, border, base + HALF)):
-                scaled[lo] = ring.tile([P, hi - lo], F32, align_bytes=64, name="scaled")
-                nc.vector.tensor_tensor(scaled[lo][:], sums[base][:, lo - base : hi - base], gain[:, lo:hi], MULT)
-            for lo, hi in pieces((base, border, base + HALF)):
-                looked_up = shift[:] if lo == HALF else beta_sb[:].indirect(entries(cls_sb, lo, hi))
-                nc.vector.tensor_tensor(shifted[:, lo:hi], looked_up, scaled[lo][:], ADD)
-                nc.scalar.activation(result[:, lo:hi], shifted[:, lo:hi], SILU)
-                nc.sync.dma_start(out[:, lo:hi], result[:, lo:hi])
+            for lo in (base, base + QUARTER):
+                scaled[lo] = ring.tile([P, QUARTER], F32, align_bytes=64, name="scaled")
+                nc.vector.tensor_tensor(scaled[lo][:], sums[base][:, lo - base : lo - base + QUARTER], gain[:, lo : lo + QUARTER], MULT)
+            for lo, hi in pieces(SUM_BORDERS):
+                if base <= lo < base + HALF:
+                    start = lo - lo % QUARTER
+                    if HALF <= lo < LAST:
+                        looked_up = shift[:, lo - HALF : hi - HALF]
+                    else:
+                        looked_up = beta_sb[:].indirect(entries(cls_sb, lo, hi))
+                    nc.vector.tensor_tensor(shifted[:, lo:hi], looked_up, scaled[start][:, lo - start : hi - start], ADD)
+                    nc.scalar.activation(result[:, lo:hi], shifted[:, lo:hi], SILU)
+                    nc.sync.dma_start(out[:, lo:hi], result[:, lo:hi])

@@ -70,10 +70,10 @@ def tile_picked_cbn_silu_p_kernel(tc, x_words, x_scales, w1, gamma, beta, offs, 
             nc.vector.tensor_copy(picked[:], scale_table[:].indirect(entries(offs_sb, lo, lo + HALF)))
             return picked
 
-        def place_scales(picked, plane):
+        def place_scales(queue, picked, plane):
             for q in range(P // QUADRANT):
                 row = P - BLOCKS + ROWS * q
-                nc.sync.dma_start(
+                queue.dma_start(
                     plane[QUADRANT * q : QUADRANT * q + ROWS, :].bitcast(I32),
                     picked[row : row + ROWS, :].bitcast(I32),
                 )
@@ -93,12 +93,12 @@ def tile_picked_cbn_silu_p_kernel(tc, x_words, x_scales, w1, gamma, beta, offs, 
             w_grouped[:].rearrange("p (c i) j -> p c j i", i=LINE), w_raw[:].rearrange("p j (c i) -> p c j i", i=LINE)
         )
         first_plane = sb.tile([P, HALF], U8, align_bytes=64)
-        place_scales(pick_scales(0), first_plane)
+        place_scales(nc.scalar, pick_scales(0), first_plane)
         late_scales = pick_scales(HALF)
         beta_sb = reuse.tile([P, U], F32, align_bytes=64, offset=TABLE_AT + HALF)
         nc.sync.dma_start(beta_sb[:], beta)
         second_plane = reuse.tile([P, HALF], U8, align_bytes=64, offset=TABLE_AT)
-        place_scales(late_scales, second_plane)
+        place_scales(nc.sync, late_scales, second_plane)
         nc.vector.quantize_mx(
             out=w_codes[:].bitcast(FP8X4), scales=w_plane[:], in_=w_grouped[:].rearrange("p m j -> p (m j)")
         )

@@ -26,12 +26,16 @@ FLOPS = 2 * K * N * S
 
 HALF = S // 2
 QUARTER = S // 4
-LAST = 896
-SUM_BORDERS = (0, 256, 512, 768, 896, 1024)
-EARLY = 640
-PRODUCT_BORDERS = (0, 256, 512, 640, 768, 1024)
-SECOND = 256
 TABLE_AT = 4 * PACK * N
+SPLIT = 512
+EARLY = 768
+PRODUCT_BORDERS = (0, 256, 512, 768, 1024)
+BANK_BORDERS = (0, 512, 1024)
+SUM_BORDERS = (0, 256, 512, 640, 768, 896, 1024)
+LAST = 896
+OWN = (256, 512)
+GAIN_PIECES = ((0, 256), (512, 1024))
+SHIFT_PIECES = ((512, 896),)
 
 
 def entries(offsets, lo, hi):
@@ -47,7 +51,6 @@ def tile_picked_cbn_silu_p_kernel(tc, x_words, x_scales, w1, gamma, beta, offs, 
     with ExitStack() as ctx:
         sb = ctx.enter_context(tc.tile_pool(name="sb", bufs=1))
         reuse = ctx.enter_context(tc.tile_pool(name="reuse", bufs=1))
-        ring = ctx.enter_context(tc.tile_pool(name="ring", bufs=2))
         psum = ctx.enter_context(tc.psum_pool(name="psum", bufs=1))
 
         offs_sb = sb.tile([P, S // STRIPE], U16)
@@ -58,16 +61,13 @@ def tile_picked_cbn_silu_p_kernel(tc, x_words, x_scales, w1, gamma, beta, offs, 
         w_grouped = sb.tile([P, N, PACK], BF16, align_bytes=64)
         w_codes = sb.tile([P, N], U32, align_bytes=64)
         w_plane = sb.tile([P, N], U8, align_bytes=64)
-        gain = sb.tile([P, S], F32, align_bytes=64)
-        shift = sb.tile([P, LAST - HALF], F32, align_bytes=64)
-        shifted = sb.tile([P, S], F32, align_bytes=64)
         result = sb.tile([P, S], F32, align_bytes=64)
         warm = sb.tile([P, 2], F32, align_bytes=64)
         w_raw = reuse.tile([P, PACK, N], F32, align_bytes=64, offset=0)
 
-        def pick_scales(lo):
-            picked = sb.tile([P, HALF], U8, align_bytes=64, name="scales%d" % lo)
-            nc.vector.tensor_copy(picked[:], scale_table[:].indirect(entries(offs_sb, lo, lo + HALF)))
+        def pick_scales(lo, hi):
+            picked = sb.tile([P, hi - lo], U8, align_bytes=64, name="scales%d" % lo)
+            nc.vector.tensor_copy(picked[:], scale_table[:].indirect(entries(offs_sb, lo, hi)))
             return picked
 
         def place_scales(queue, picked, plane):
@@ -92,12 +92,12 @@ def tile_picked_cbn_silu_p_kernel(tc, x_words, x_scales, w1, gamma, beta, offs, 
         nc.scalar.copy(
             w_grouped[:].rearrange("p (c i) j -> p c j i", i=LINE), w_raw[:].rearrange("p j (c i) -> p c j i", i=LINE)
         )
-        first_plane = sb.tile([P, HALF], U8, align_bytes=64)
-        place_scales(nc.scalar, pick_scales(0), first_plane)
-        late_scales = pick_scales(HALF)
+        first_plane = sb.tile([P, SPLIT], U8, align_bytes=64)
+        place_scales(nc.scalar, pick_scales(0, SPLIT), first_plane)
+        late_scales = pick_scales(SPLIT, S)
         beta_sb = reuse.tile([P, U], F32, align_bytes=64, offset=TABLE_AT + HALF)
         nc.sync.dma_start(beta_sb[:], beta)
-        second_plane = reuse.tile([P, HALF], U8, align_bytes=64, offset=TABLE_AT)
+        second_plane = reuse.tile([P, S - SPLIT], U8, align_bytes=64, offset=TABLE_AT)
         place_scales(nc.sync, late_scales, second_plane)
         nc.vector.quantize_mx(
             out=w_codes[:].bitcast(FP8X4), scales=w_plane[:], in_=w_grouped[:].rearrange("p m j -> p (m j)")
@@ -107,12 +107,17 @@ def tile_picked_cbn_silu_p_kernel(tc, x_words, x_scales, w1, gamma, beta, offs, 
         nc.vector.tensor_copy(early_words[:], word_table[:].bitcast(U32).indirect(entries(offs_sb, 0, EARLY)))
         late_words = reuse.tile([P, S - EARLY], U32, align_bytes=64, offset=0)
         nc.vector.tensor_copy(late_words[:], word_table[:].bitcast(U32).indirect(entries(offs_sb, EARLY, S)))
-        sums = {0: psum.tile([P, HALF], F32, name="first_sums"), HALF: psum.tile([P, HALF], F32, name="second_sums")}
+        banks = {lo: psum.tile([P, hi - lo], F32, name="sums%d" % lo) for lo, hi in pieces(BANK_BORDERS)}
+
+        def sums(lo, hi):
+            start = max(b for b in banks if b <= lo)
+            return banks[start][:, lo - start : hi - start]
+
         for lo, hi in pieces(PRODUCT_BORDERS):
-            base, plane = (0, first_plane) if lo < HALF else (HALF, second_plane)
+            base, plane = (0, first_plane) if lo < SPLIT else (SPLIT, second_plane)
             words = early_words[:, lo:hi] if lo < EARLY else late_words[:, lo - EARLY : hi - EARLY]
             nc.tensor.matmul_mx(
-                out=sums[base][:, lo - base : hi - base],
+                out=sums(lo, hi),
                 lhsT=w_codes[:].bitcast(FP8X4),
                 lhsT_scale=w_plane[:],
                 rhs=words.bitcast(FP8X4),
@@ -120,23 +125,32 @@ def tile_picked_cbn_silu_p_kernel(tc, x_words, x_scales, w1, gamma, beta, offs, 
                 start=True,
                 stop=True,
             )
-        nc.vector.tensor_copy(gain[:, SECOND:HALF], gamma_sb[:].indirect(entries(cls_sb, SECOND, HALF)))
-        for lo, hi in ((0, SECOND), (HALF, S)):
-            nc.scalar.activation(gain[:, lo:hi], gamma_sb[:].indirect(entries(cls_sb, lo, hi)), COPY)
-        nc.scalar.activation(shift[:], beta_sb[:].indirect(entries(cls_sb, HALF, LAST)), COPY)
+
+        def gamma_of(lo, hi):
+            return gamma_sb[:].indirect(entries(cls_sb, lo, hi))
+
+        def beta_of(lo, hi):
+            return beta_sb[:].indirect(entries(cls_sb, lo, hi))
+
+        gain = sb.tile([P, S], F32, align_bytes=64)
+        shift = sb.tile([P, LAST - HALF], F32, align_bytes=64)
+        shifted = sb.tile([P, S], F32, align_bytes=64)
+        ring = ctx.enter_context(tc.tile_pool(name="ring", bufs=2))
+        nc.vector.tensor_copy(gain[:, OWN[0] : OWN[1]], gamma_of(*OWN))
+        for lo, hi in GAIN_PIECES:
+            nc.scalar.activation(gain[:, lo:hi], gamma_of(lo, hi), COPY)
+        for lo, hi in SHIFT_PIECES:
+            nc.scalar.activation(shift[:, lo - HALF : hi - HALF], beta_of(lo, hi), COPY)
 
         for base in (0, HALF):
             scaled = {}
             for lo in (base, base + QUARTER):
                 scaled[lo] = ring.tile([P, QUARTER], F32, align_bytes=64, name="scaled")
-                nc.vector.tensor_tensor(scaled[lo][:], sums[base][:, lo - base : lo - base + QUARTER], gain[:, lo : lo + QUARTER], MULT)
+                nc.vector.tensor_tensor(scaled[lo][:], sums(lo, lo + QUARTER), gain[:, lo : lo + QUARTER], MULT)
             for lo, hi in pieces(SUM_BORDERS):
                 if base <= lo < base + HALF:
                     start = lo - lo % QUARTER
-                    if HALF <= lo < LAST:
-                        looked_up = shift[:, lo - HALF : hi - HALF]
-                    else:
-                        looked_up = beta_sb[:].indirect(entries(cls_sb, lo, hi))
+                    looked_up = shift[:, lo - HALF : hi - HALF] if HALF <= lo < LAST else beta_of(lo, hi)
                     nc.vector.tensor_tensor(shifted[:, lo:hi], looked_up, scaled[start][:, lo - start : hi - start], ADD)
                     nc.scalar.activation(result[:, lo:hi], shifted[:, lo:hi], SILU)
                     nc.sync.dma_start(out[:, lo:hi], result[:, lo:hi])

@@ -31,11 +31,9 @@ SPLIT = 512
 EARLY = 768
 PRODUCT_BORDERS = (0, 256, 512, 768, 1024)
 BANK_BORDERS = (0, 512, 1024)
-SUM_BORDERS = (0, 256, 512, 640, 768, 896, 1024)
-LAST = 896
-OWN = (256, 512)
-GAIN_PIECES = ((0, 256), (512, 1024))
-SHIFT_PIECES = ((512, 896),)
+OWN = (256, 640)
+GAIN_PIECES = ((0, 256), (640, 1024))
+EIGHTH = S // 8
 
 
 def entries(offsets, lo, hi):
@@ -133,24 +131,46 @@ def tile_picked_cbn_silu_p_kernel(tc, x_words, x_scales, w1, gamma, beta, offs, 
             return beta_sb[:].indirect(entries(cls_sb, lo, hi))
 
         gain = sb.tile([P, S], F32, align_bytes=64)
-        shift = sb.tile([P, LAST - HALF], F32, align_bytes=64)
         shifted = sb.tile([P, S], F32, align_bytes=64)
         ring = ctx.enter_context(tc.tile_pool(name="ring", bufs=2))
+        narrow = ctx.enter_context(tc.tile_pool(name="narrow", bufs=1))
         nc.vector.tensor_copy(gain[:, OWN[0] : OWN[1]], gamma_of(*OWN))
         for lo, hi in GAIN_PIECES:
             nc.scalar.activation(gain[:, lo:hi], gamma_of(lo, hi), COPY)
-        for lo, hi in SHIFT_PIECES:
-            nc.scalar.activation(shift[:, lo - HALF : hi - HALF], beta_of(lo, hi), COPY)
 
-        for base in (0, HALF):
-            scaled = {}
-            for lo in (base, base + QUARTER):
-                scaled[lo] = ring.tile([P, QUARTER], F32, align_bytes=64, name="scaled")
-                nc.vector.tensor_tensor(scaled[lo][:], sums(lo, lo + QUARTER), gain[:, lo : lo + QUARTER], MULT)
-            for lo, hi in pieces(SUM_BORDERS):
-                if base <= lo < base + HALF:
-                    start = lo - lo % QUARTER
-                    looked_up = shift[:, lo - HALF : hi - HALF] if HALF <= lo < LAST else beta_of(lo, hi)
-                    nc.vector.tensor_tensor(shifted[:, lo:hi], looked_up, scaled[start][:, lo - start : hi - start], ADD)
-                    nc.scalar.activation(result[:, lo:hi], shifted[:, lo:hi], SILU)
-                    nc.sync.dma_start(out[:, lo:hi], result[:, lo:hi])
+        def look_up(pool, lo, hi):
+            shift = pool.tile([P, hi - lo], F32, align_bytes=64, name="shift")
+            nc.scalar.activation(shift[:], beta_of(lo, hi), COPY)
+            return shift
+
+        def scale(lo):
+            scaled = ring.tile([P, QUARTER], F32, align_bytes=64, name="scaled")
+            nc.vector.tensor_tensor(scaled[:], sums(lo, lo + QUARTER), gain[:, lo : lo + QUARTER], MULT)
+            return scaled
+
+        def add(lo, looked_up, scaled, width=EIGHTH):
+            at = lo % QUARTER
+            nc.vector.tensor_tensor(shifted[:, lo : lo + width], looked_up, scaled[:, at : at + width], ADD)
+
+        def store(lo, hi):
+            nc.scalar.activation(result[:, lo:hi], shifted[:, lo:hi], SILU)
+            nc.sync.dma_start(out[:, lo:hi], result[:, lo:hi])
+
+        early_shift = look_up(narrow, 3 * EIGHTH, HALF)
+        wide_shift = look_up(sb, HALF, HALF + QUARTER)
+        first, second = scale(0), scale(QUARTER)
+        add(0, beta_of(0, QUARTER), first, QUARTER)
+        store(0, QUARTER)
+        add(QUARTER, beta_of(QUARTER, 3 * EIGHTH), second)
+        add(3 * EIGHTH, early_shift[:], second)
+        store(QUARTER, HALF)
+        late_shift = look_up(narrow, 7 * EIGHTH, S)
+        third, fourth = scale(HALF), scale(HALF + QUARTER)
+        for lo, looked_up, scaled in (
+            (HALF, wide_shift[:, 0:EIGHTH], third),
+            (5 * EIGHTH, wide_shift[:, EIGHTH:QUARTER], third),
+            (6 * EIGHTH, beta_of(6 * EIGHTH, 7 * EIGHTH), fourth),
+            (7 * EIGHTH, late_shift[:], fourth),
+        ):
+            add(lo, looked_up, scaled)
+            store(lo, lo + EIGHTH)

@@ -31,8 +31,8 @@ SPLIT = 512
 EARLY = 768
 PRODUCT_BORDERS = (0, 256, 512, 768, 1024)
 BANK_BORDERS = (0, 512, 1024)
-OWN = (256, 640)
-GAIN_PIECES = ((0, 256), (640, 1024))
+OWN = (256, 576)
+GAIN_PIECES = ((0, 256), (576, 1024))
 EIGHTH = S // 8
 
 

@@ -31,8 +31,8 @@ SPLIT = 512
 EARLY = 768
 PRODUCT_BORDERS = (0, 256, 512, 768, 1024)
 BANK_BORDERS = (0, 512, 1024)
-OWN = (256, 576)
-GAIN_PIECES = ((0, 256), (576, 1024))
+OWN = (256, 512)
+GAIN_PIECES = ((0, 256), (512, 1024))
 EIGHTH = S // 8
 
 

from contextlib import ExitStack

import concourse.mybir as mybir

F32 = mybir.dt.float32
BF16 = mybir.dt.bfloat16
I32 = mybir.dt.int32
U32 = mybir.dt.uint32
U16 = mybir.dt.uint16
U8 = mybir.dt.uint8
FP8X4 = mybir.dt.float8_e4m3fn_x4
MULT = mybir.AluOpType.mult
ADD = mybir.AluOpType.add
COPY = mybir.ActivationFunctionType.Copy
SILU = mybir.ActivationFunctionType.Silu

P = 128
PACK = 4
K, T, S, N, U = 512, 2048, 1024, 128, 1024
STRIPE = 16
BLOCKS = K // 32
QUADRANT = 32
ROWS = BLOCKS * QUADRANT // P
LINE = 4
FLOPS = 2 * K * N * S

HALF = S // 2
QUARTER = S // 4
TABLE_AT = 4 * PACK * N
SPLIT = 512
EARLY = 768
PRODUCT_BORDERS = (0, 256, 512, 768, 1024)
BANK_BORDERS = (0, 512, 1024)
OWN = (256, 512)
GAIN_PIECES = ((0, 256), (512, 1024))
EIGHTH = S // 8


def entries(offsets, lo, hi):
    return offsets[:, lo // STRIPE : hi // STRIPE]


def pieces(borders):
    return list(zip(borders[:-1], borders[1:]))


def tile_picked_cbn_silu_p_kernel(tc, x_words, x_scales, w1, gamma, beta, offs, cls, out):
    nc = tc.nc
    with ExitStack() as ctx:
        sb = ctx.enter_context(tc.tile_pool(name="sb", bufs=1))
        reuse = ctx.enter_context(tc.tile_pool(name="reuse", bufs=1))
        psum = ctx.enter_context(tc.psum_pool(name="psum", bufs=1))

        offs_sb = sb.tile([P, S // STRIPE], U16)
        cls_sb = sb.tile([P, S // STRIPE], U16)
        scale_table = reuse.tile([P, T], U8, align_bytes=64, offset=TABLE_AT)
        word_table = sb.tile([P, T], I32, align_bytes=64)
        gamma_sb = sb.tile([P, U], F32, align_bytes=64)
        w_grouped = sb.tile([P, N, PACK], BF16, align_bytes=64)
        w_codes = sb.tile([P, N], U32, align_bytes=64)
        w_plane = sb.tile([P, N], U8, align_bytes=64)
        result = sb.tile([P, S], F32, align_bytes=64)
        warm = sb.tile([P, 2], F32, align_bytes=64)
        w_raw = reuse.tile([P, PACK, N], F32, align_bytes=64, offset=0)

        def pick_scales(lo, hi):
            picked = sb.tile([P, hi - lo], U8, align_bytes=64, name="scales%d" % lo)
            nc.vector.tensor_copy(picked[:], scale_table[:].indirect(entries(offs_sb, lo, hi)))
            return picked

        def place_scales(queue, picked, plane):
            for q in range(P // QUADRANT):
                row = P - BLOCKS + ROWS * q
                queue.dma_start(
                    plane[QUADRANT * q : QUADRANT * q + ROWS, :].bitcast(I32),
                    picked[row : row + ROWS, :].bitcast(I32),
                )

        nc.gpsimd.memset(warm[:, 0:1], 0.0)
        nc.scalar.activation(warm[:, 1:2], warm[:, 0:1], SILU)

        nc.sync.dma_start(scale_table[P - BLOCKS : P, :].bitcast(I32), x_scales[0].bitcast(I32))
        nc.sync.dma_start(offs_sb[:], offs)
        nc.vector.memset(scale_table[0 : P - BLOCKS, :].bitcast(I32), 0)
        nc.sync.dma_start(word_table[:], x_words[0].rearrange("p c t -> p (c t)").bitcast(I32))
        nc.sync.dma_start(w_raw[:], w1.rearrange("(p j) m -> p j m", j=PACK))
        nc.sync.dma_start(cls_sb[:], cls)
        nc.sync.dma_start(gamma_sb[:], gamma)

        nc.scalar.copy(
            w_grouped[:].rearrange("p (c i) j -> p c j i", i=LINE), w_raw[:].rearrange("p j (c i) -> p c j i", i=LINE)
        )
        first_plane = sb.tile([P, SPLIT], U8, align_bytes=64)
        place_scales(nc.scalar, pick_scales(0, SPLIT), first_plane)
        late_scales = pick_scales(SPLIT, S)
        beta_sb = reuse.tile([P, U], F32, align_bytes=64, offset=TABLE_AT + HALF)
        nc.sync.dma_start(beta_sb[:], beta)
        second_plane = reuse.tile([P, S - SPLIT], U8, align_bytes=64, offset=TABLE_AT)
        place_scales(nc.sync, late_scales, second_plane)
        nc.vector.quantize_mx(
            out=w_codes[:].bitcast(FP8X4), scales=w_plane[:], in_=w_grouped[:].rearrange("p m j -> p (m j)")
        )

        early_words = sb.tile([P, EARLY], U32, align_bytes=64)
        nc.vector.tensor_copy(early_words[:], word_table[:].bitcast(U32).indirect(entries(offs_sb, 0, EARLY)))
        late_words = reuse.tile([P, S - EARLY], U32, align_bytes=64, offset=0)
        nc.vector.tensor_copy(late_words[:], word_table[:].bitcast(U32).indirect(entries(offs_sb, EARLY, S)))
        banks = {lo: psum.tile([P, hi - lo], F32, name="sums%d" % lo) for lo, hi in pieces(BANK_BORDERS)}

        def sums(lo, hi):
            start = max(b for b in banks if b <= lo)
            return banks[start][:, lo - start : hi - start]

        for lo, hi in pieces(PRODUCT_BORDERS):
            base, plane = (0, first_plane) if lo < SPLIT else (SPLIT, second_plane)
            words = early_words[:, lo:hi] if lo < EARLY else late_words[:, lo - EARLY : hi - EARLY]
            nc.tensor.matmul_mx(
                out=sums(lo, hi),
                lhsT=w_codes[:].bitcast(FP8X4),
                lhsT_scale=w_plane[:],
                rhs=words.bitcast(FP8X4),
                rhs_scale=plane[:, lo - base : hi - base],
                start=True,
                stop=True,
            )

        def gamma_of(lo, hi):
            return gamma_sb[:].indirect(entries(cls_sb, lo, hi))

        def beta_of(lo, hi):
            return beta_sb[:].indirect(entries(cls_sb, lo, hi))

        gain = sb.tile([P, S], F32, align_bytes=64)
        shifted = sb.tile([P, S], F32, align_bytes=64)
        ring = ctx.enter_context(tc.tile_pool(name="ring", bufs=2))
        narrow = ctx.enter_context(tc.tile_pool(name="narrow", bufs=1))
        nc.vector.tensor_copy(gain[:, OWN[0] : OWN[1]], gamma_of(*OWN))
        for lo, hi in GAIN_PIECES:
            nc.scalar.activation(gain[:, lo:hi], gamma_of(lo, hi), COPY)

        def look_up(pool, lo, hi):
            shift = pool.tile([P, hi - lo], F32, align_bytes=64, name="shift")
            nc.scalar.activation(shift[:], beta_of(lo, hi), COPY)
            return shift

        def scale(lo):
            scaled = ring.tile([P, QUARTER], F32, align_bytes=64, name="scaled")
            nc.vector.tensor_tensor(scaled[:], sums(lo, lo + QUARTER), gain[:, lo : lo + QUARTER], MULT)
            return scaled

        def add(lo, looked_up, scaled, width=EIGHTH):
            at = lo % QUARTER
            nc.vector.tensor_tensor(shifted[:, lo : lo + width], looked_up, scaled[:, at : at + width], ADD)

        def store(lo, hi):
            nc.scalar.activation(result[:, lo:hi], shifted[:, lo:hi], SILU)
            nc.sync.dma_start(out[:, lo:hi], result[:, lo:hi])

        early_shift = look_up(narrow, 3 * EIGHTH, HALF)
        wide_shift = look_up(sb, HALF, HALF + QUARTER)
        first, second = scale(0), scale(QUARTER)
        add(0, beta_of(0, QUARTER), first, QUARTER)
        store(0, QUARTER)
        add(QUARTER, beta_of(QUARTER, 3 * EIGHTH), second)
        add(3 * EIGHTH, early_shift[:], second)
        store(QUARTER, HALF)
        late_shift = look_up(narrow, 7 * EIGHTH, S)
        third, fourth = scale(HALF), scale(HALF + QUARTER)
        for lo, looked_up, scaled in (
            (HALF, wide_shift[:, 0:EIGHTH], third),
            (5 * EIGHTH, wide_shift[:, EIGHTH:QUARTER], third),
            (6 * EIGHTH, beta_of(6 * EIGHTH, 7 * EIGHTH), fourth),
            (7 * EIGHTH, late_shift[:], fourth),
        ):
            add(lo, looked_up, scaled)
            store(lo, lo + EIGHTH)
